import numpy as np, ml_dtypes
CORES = [3,7,11,15,131,135,139,143]
N = 8
BF = ml_dtypes.bfloat16
B, W, CAP, RO = 1024, 3200, 32, 3
L = N * CAP
def parts(rng):
    share = rng.choice(np.array([0.1, 0.2, 0.4, 0.6]), (N, 8, 1, B))
    v = np.where(rng.random((N, 8, 16, B)) < share, -rng.integers(1, 256, (N, 8, 16, B)), rng.integers(0, 256, (N, 8, 16, B)))
    a = rng.integers(0, 256, (N, 8, 16, W)) * (rng.random((N, 8, 16, W)) < rng.choice(np.array([0.3, 0.6, 0.9]), (N, 8, 1, W))); a[..., W - 1] = 0
    u = rng.integers(0, W - 1, (N, 8, 16, B))
    u = np.where(rng.random(u.shape) < rng.choice(np.array([0.0, 0.0, 0.1, 0.1, 0.4, 0.96]), (N, 8, 1, B)), W - 1, u)
    to = np.where(rng.random((N, 8, W)) < rng.choice(np.array([0.0, 0.1, 0.25]), (N, 8, 1)), rng.integers(0, N, (N, 8, 1)), rng.integers(0, N, (N, 8, W)))
    pay = to * B + rng.integers(0, B, (N, 8, W))
    wk = np.where(rng.random((N, 8, L)) < 0.04, B, rng.integers(0, B, (N, 8, L)))
    return v, a, u, pay, wk
def pack(v, a, u, pay, wk):
    return {"vp": np.ascontiguousarray(v.reshape(N, 128, B)).astype(np.float32).astype(BF), "am": np.ascontiguousarray(a.reshape(N, 128, W)).astype(np.float32).astype(BF),
            "qu": np.ascontiguousarray(u.reshape(N, 128, B)).astype(np.int32), "pay": np.ascontiguousarray(pay).astype(np.int32), "wk": np.ascontiguousarray(wk).astype(np.int32)}
def setup_inputs(rng):
    return pack(*parts(rng))
def plant(rng, v, a, u, pay, wk, q, g, to):
    m = len(to); lanes = rng.permutation(L)[:m]; banks = rng.permutation(B)[:m]; lines = rng.permutation(W - 1)[:m]
    row = rng.integers(0, 16, m); j = rng.integers(0, 16, m)
    u[q, g][:, banks] = W - 1; u[q, g][row, banks] = lines
    v[q, g][j, banks] = -rng.integers(1, 256, m); a[q, g][j, lines] = 255
    order = np.argsort(lanes); pay[q, g][lines[order]] = to
    wk[q, g] = B; wk[q, g][lanes] = banks
def setup_inputs_room(rng):
    v, a, u, pay, wk = parts(rng)
    for q in range(N):
        for g in range(8):
            cnt = [CAP, CAP + 1, CAP - 1, 0, 1, 0, 2, CAP // 2][:N]
            if (q + g) % 4 == 3: cnt = [L] + [0] * (N - 1)
            to = np.concatenate([np.full(n, (q + 1 + g + j) % N, np.int64) for j, n in enumerate(cnt)])
            plant(rng, v, a, u, pay, wk, q, g, rng.permutation(to) * B + rng.integers(0, B, len(to)))
    return pack(v, a, u, pay, wk)
def setup_inputs_ties(rng):
    v, a, u, pay, wk = parts(rng)
    v[:, ::2] = rng.integers(-3, 3, (N, 4, 16, B)); a[:, ::2] = rng.integers(0, 4, (N, 4, 16, W))
    v[:, 1::2] = rng.integers(-3, 2, (N, 4, 16, B)) * 85; a[:, 1::2] = rng.integers(0, 4, (N, 4, 16, W)) * 85
    a = a * (rng.random((N, 8, 1, W)) < 0.6); a[..., W - 1] = 0
    u[:, :, 15] = np.where(rng.random((N, 8, B)) < 0.4, W - 1, u[:, :, 15])
    return pack(v, a, u, pay, wk)
def setup_inputs_alike(rng):
    v, a, u, pay, wk = parts(rng)
    wk[:, 0] = rng.choice(np.array([0, B - 1, 5, B // 2]), (N, L))
    u[:, 2] = rng.choice(np.array([0, W - 2, 7, W // 2, W - 1]), (N, 16, B))
    pay[:, 4] = rng.integers(0, N, (N, W)) * B + rng.choice(np.array([0, B - 1]), (N, W))
    u[:, 6] = np.repeat(u[:, 6, :1], 16, axis=1)
    wk[:, 1::2, L - 1] = wk[:, 1::2, 0]
    return pack(v, a, u, pay, wk)
def setup_inputs_dry(rng):
    v, a, u, pay, wk = parts(rng); o = rng.permutation(8)
    wk[:, o[0]] = B; a[:, o[1]] = 0; u[:, o[2]] = W - 1; v[:, o[3]] = np.abs(v[:, o[3]])
    v[:, o[4]] = -255; a[:, o[4]] = 255; a[..., W - 1] = 0
    wk[rng.integers(0, N), o[5]] = B
    h = int(o[6]); wk[:, h] = B
    for q in range(N):
        b = int(rng.integers(1, B)); n, m = [int(i) for i in rng.permutation(W - 1)[:2]]
        wk[q, h, int(rng.integers(0, L))] = b
        v[q, h, :, b] = -rng.integers(1, 256, 16); u[q, h, :, b] = n; a[q, h, :, n] = 0; pay[q, h, n] = (q + 1) % N * B
        v[q, h, :, 0] = -rng.integers(1, 256, 16); u[q, h, :, 0] = m; a[q, h, :, m] = 255; pay[q, h, m] = rng.integers(0, N) * B + rng.integers(1, B)
    return pack(v, a, u, pay, wk)
def setup_inputs_spread(rng):
    v, a, u, pay, wk = parts(rng)
    v = (np.exp2(8 * rng.random((N, 8, 1, B))) * rng.random((N, 8, 16, B))).astype(np.int64) * np.where(rng.random((N, 8, 16, B)) < 0.4, -1, 1)
    a = (np.exp2(8 * rng.random((N, 8, 1, W))) * rng.random((N, 8, 16, W))).astype(np.int64); a[..., W - 1] = 0
    u = np.where(u == W - 1, u, ((W - 1) * rng.random(u.shape) ** 2).astype(np.int64))
    pay = pay // B * B + (B * rng.random(pay.shape) ** 2).astype(np.int64)
    wk = np.where(wk == B, B, (B * rng.random(wk.shape) ** 2).astype(np.int64))
    return pack(v, a, u, pay, wk)
def check_inputs(d):
    bad = []
    for k, lo, hi in (("vp", -255, 255), ("am", 0, 255)):
        x = np.asarray(d[k]).astype(np.float32)
        if not np.all((x >= lo) & (x <= hi)): bad.append("range of " + k)
        elif not np.all(x == np.rint(x)): bad.append("whole numbers in " + k)
    if not np.all(np.asarray(d["am"]).astype(np.float32)[..., W - 1] == 0): bad.append("zeros in the last column of am")
    for k, hi in (("qu", W - 1), ("pay", N * B - 1), ("wk", B)):
        if np.min(d[k]) < 0 or np.max(d[k]) > hi: bad.append("range of " + k)
    return bad
def reference(vp, am, qu, pay, wk):
    v = vp.astype(np.float32).astype(np.int64).reshape(N, 8, 16, B); a = am.astype(np.float32).astype(np.int64).reshape(N, 8, 16, W)
    u = qu.astype(np.int64).reshape(N, 8, 16, B); payee = pay.astype(np.int64)
    w = wk.astype(np.int64); c = np.zeros((N, 8, 16, L), np.int64)
    for rnd in range(RO):
        w2 = np.full((N, 8, L), B, np.int64); c2 = np.zeros((N, 8, 16, L), np.int64)
        for q in range(N):
            for g in range(8):
                vv, aa, uu = v[q, g], a[q, g], u[q, g]
                lane = np.nonzero(w[q, g] < B)[0]
                lane = lane[np.sort(np.unique(w[q, g][lane], return_index=True)[1])]
                b = w[q, g][lane]
                x = np.maximum(vv[:, b] - c[q, g][:, lane], -255); vv[:, b] = x
                keep = np.any(x < 0, axis=0); b, x = b[keep], x[:, keep]
                n = uu[:, b]
                score = np.sum(x[:, None, :] + aa[:, n] >= 0, axis=0)
                best = 15 - np.argmax(score[::-1], axis=0)
                p = n[best, np.arange(len(b))]
                keep = p != W - 1; b, x, best, p = b[keep], x[:, keep], best[keep], p[keep]
                keep = np.sort(np.unique(p, return_index=True)[1]); b, x, best, p = b[keep], x[:, keep], best[keep], p[keep]
                t = np.minimum(aa[:, p], np.maximum(-x, 0))
                vv[:, b] = x + t; aa[:, p] = aa[:, p] - t; uu[best, b] = W - 1
                to = payee[q, g][p]
                for r in range(N):
                    k = np.nonzero(to // B == r)[0][:CAP]; s = q * CAP + np.arange(len(k))
                    w2[r, g][s] = to[k] % B; c2[r, g][:, s] = t[:, k]
        w, c = w2, c2
    return {"yv": v.reshape(N, 128, B).astype(np.float32).astype(BF), "yw": w.astype(np.float32), "yc": c.reshape(N, 128, L).astype(np.float32).astype(BF)}

@@ -1,0 +1,466 @@
+from concourse.bass import DstId, RemoteDMATransfer
+from concourse.mybir import AluOpType as O, ActivationFunctionType as F
+
+WIN = 2312
+SCRATCH = {
+    "wkb": ("sbuf", [128, 256], "int32"), "wkf": ("sbuf", [128, 256], "float32"), "xz": ("sbuf", [128, 256], "float32"),
+    "quS": ("sbuf", [128, 1024], "int32"), "ut": ("sbuf", [128, 1296], "float32"), "vt": ("sbuf", [128, 1296], "bfloat16"),
+    "at": ("sbuf", [128, 3456], "bfloat16"), "pt": ("sbuf", [128, 3200], "int32"),
+    "mi": ("sbuf", [128, 256], "int32"), "l4": ("sbuf", [128, 256], "int32"), "l15": ("sbuf", [128, 256], "int32"),
+    "pci": ("sbuf", [128, 8], "int32"), "col": ("sbuf", [128, 32], "float32"), "l16": ("sbuf", [128, 16], "int32"),
+    "dumpA": ("sbuf", [128, 16], "float32"), "dumpB": ("sbuf", [128, 16], "float32"),
+    "maskS": ("sbuf", [128, 256], "bfloat16"), "rst": ("sbuf", [128, 256], "bfloat16"), "ones": ("sbuf", [128, 256], "bfloat16"),
+    "blk1": ("sbuf", [128, 128], "bfloat16"), "blk8": ("sbuf", [128, 128], "bfloat16"), "woff": ("sbuf", [128, 128], "bfloat16"),
+    "bs1": ("sbuf", [128, 8], "bfloat16"), "bs64": ("sbuf", [128, 8], "bfloat16"),
+    "idF": ("sbuf", [128, 128], "float32"), "idB": ("sbuf", [128, 128], "bfloat16"), "sel8": ("sbuf", [128, 128], "float32"),
+    "selx": ("sbuf", [128, 768], "bfloat16"),
+    "ci": ("sbuf", [128, 256], "int32"), "xi": ("sbuf", [128, 256], "int32"), "cI": ("sbuf", [128, 256], "int32"),
+    "M1": ("sbuf", [128, 256], "float32"), "M5": ("sbuf", [128, 256], "float32"), "M6": ("sbuf", [128, 256], "float32"), "M7": ("sbuf", [128, 256], "float32"),
+    "SC5": ("sbuf", [128, 256], "float32"), "SC6": ("sbuf", [128, 256], "float32"), "SC7": ("sbuf", [128, 256], "float32"),
+    "BWu": ("sbuf", [128, 16], "uint16"), "LWu": ("sbuf", [128, 16], "uint16"), "OWu": ("sbuf", [128, 16], "uint16"),
+    "boU": ("sbuf", [128, 16], "uint16"), "aoU": ("sbuf", [128, 16], "uint16"), "sm": ("sbuf", [128, 128], "float32"),
+    "xu": ("sbuf", [128, 256], "uint16"), "Lu": ("sbuf", [128, 256], "uint16"), "Uo": ("sbuf", [128, 256], "uint16"),
+    "UI": ("sbuf", [128, 256], "float32"), "V1": ("sbuf", [128, 256], "bfloat16"), "V2": ("sbuf", [128, 256], "bfloat16"),
+    "neg": ("sbuf", [128, 256], "bfloat16"), "NVr": ("sbuf", [128, 256], "bfloat16"), "NVx": ("sbuf", [128, 2048], "bfloat16"),
+    "eqx": ("sbuf", [128, 3840], "bfloat16"), "eqd": ("sbuf", [128, 256], "bfloat16"),
+    "ge0": ("sbuf", [128, 2048], "bfloat16"), "Ag": ("sbuf", [128, 2048], "bfloat16"), "ge1": ("sbuf", [128, 2048], "bfloat16"),
+    "so": ("sbuf", [128, 128], "float32"), "m1": ("sbuf", [128, 128], "float32"), "m2": ("sbuf", [128, 64], "float32"),
+    "m3": ("sbuf", [128, 32], "float32"), "m4": ("sbuf", [128, 16], "float32"),
+    "ki": ("sbuf", [128, 16], "int32"), "digI": ("sbuf", [128, 48], "int32"), "digB": ("sbuf", [128, 64], "bfloat16"),
+    "TTs": ("sbuf", [128, 128], "bfloat16"),
+    "tt": ("sbuf", [128, 256], "bfloat16"), "t16": ("sbuf", [128, 256], "float32"), "Agl": ("sbuf", [128, 256], "bfloat16"),
+    "payf": ("sbuf", [128, 256], "float32"), "r8": ("sbuf", [128, 256], "int32"), "zz": ("sbuf", [128, 256], "bfloat16"),
+    "OH": ("sbuf", [128, 256], "bfloat16"), "prod": ("sbuf", [128, 256], "bfloat16"),
+    "tm": ("sbuf", [128, 256], "bfloat16"), "Vn": ("sbuf", [128, 256], "bfloat16"), "An": ("sbuf", [128, 256], "bfloat16"),
+    "OHu": ("sbuf", [128, 256], "float32"), "OHk": ("sbuf", [128, 256], "float32"), "UIn": ("sbuf", [128, 256], "float32"),
+    "ycS": ("sbuf", [128, 256], "bfloat16"), "ywS": ("sbuf", [128, 256], "float32"),
+}
+for _s in range(3):
+    SCRATCH["win%d" % _s] = ("sbuf", [128, WIN], "float32")
+    SCRATCH["land%d" % _s] = ("sbuf", [128, 256], "float32")
+for _s in range(8):
+    SCRATCH["b%d" % _s] = ("psum", [128, 512], "float32")
+SEMAPHORES = ["sv", "ss", "sp", "sg", "dwk", "dvp", "dqu", "dam", "dpay", "dyv", "dyw", "dyc", "loc", "arr0", "arr1", "arr2"]
+NONE1 = 3200
+XKEY = 272 * 4096 + NONE1
+BIGW = WIN
+
+
+def A(name, c0, c1, step=1, p0=0, p1=128):
+    return ("A", name, c0, c1, step, p0, p1)
+
+
+def IND(win, off):
+    return ("I", win, off)
+
+
+def is_view(x):
+    return isinstance(x, tuple) and len(x) > 0 and (x[0] == "A" or x[0] == "I")
+
+
+class Plan:
+    def setup(self, g, T):
+        return {"g": g, "T": T, "hist": {}, "known": {q: {} for q in "vspyg"}, "cnt": {"sv": 0, "ss": 0, "sp": 0, "sg": 0},
+                "eng": {"v": g.vector, "s": g.scalar, "p": g.tensor, "y": g.sync, "g": g}}
+
+
+def hits(a, b):
+    if a[2] <= b[1] or b[2] <= a[1]:
+        return False
+    if a[3] > 1 and a[3] == b[3] and (a[1] - b[1]) % a[3] != 0:
+        return False
+    return True
+
+
+def is_psum(name):
+    return len(name) == 2 and name[0] == "b"
+
+
+def resolve(P, x):
+    if x[0] == "I":
+        return resolve(P, x[1]).indirect(resolve(P, x[2]))
+    t = P["T"][x[1]]
+    if x[4] == 1:
+        return t[x[5]:x[6], x[2]:x[3]]
+    return t[x[5]:x[6], x[2]:x[3]:x[4]]
+
+
+def regions(views):
+    out = []
+    for v in views:
+        if v[0] == "I":
+            out += regions([v[1], v[2]])
+        else:
+            out.append((v[1], v[2], v[3], v[4]))
+    return out
+
+
+def sync_for(P, q, reads, writes):
+    need = []
+    for kind, regs in (("r", reads), ("w", writes)):
+        for r in regs:
+            ps = is_psum(r[0])
+            for h in P["hist"].get(r[0], []):
+                hk, hr, hq, sem, val, clock = h
+                same = hq == q
+                if ps and not same:
+                    pass
+                else:
+                    if kind == "r" and hk == "r":
+                        continue
+                    if same and (kind == "w" and hk == "r"):
+                        continue
+                    if same and kind == "w" and q == "p":
+                        continue
+                    if not hits(r, hr):
+                        continue
+                need.append((sem, val, clock))
+    best = {}
+    for sem, val, clock in need:
+        if P["known"][q].get(sem, 0) < val and (sem not in best or best[sem][0] < val):
+            best[sem] = (val, clock)
+    for sem in list(best):
+        val = best[sem][0]
+        if any(s2 != sem and best[s2][1].get(sem, 0) >= val for s2 in best):
+            del best[sem]
+    for sem in best:
+        val, clock = best[sem]
+        P["eng"][q].wait_ge(P["T"].sem[sem], val)
+        k = P["known"][q]
+        for s2, v2 in clock.items():
+            if k.get(s2, 0) < v2:
+                k[s2] = v2
+
+
+def note(P, q, reads, writes, sem, val):
+    clock = dict(P["known"].get(q, {}))
+    clock[sem] = max(val, clock.get(sem, 0))
+    for kind, regs in (("r", reads), ("w", writes)):
+        for r in regs:
+            lst = P["hist"].setdefault(r[0], [])
+            if kind == "w" and r[3] == 1:
+                lst[:] = [h for h in lst if not (r[1] <= h[1][1] and h[1][2] <= r[2] and (h[2] == q or h[0] == "r" or not is_psum(r[0])) and h[2] == q)]
+            lst.append((kind, r, q, sem, val, clock))
+
+
+SEM_OF = {"v": "sv", "s": "ss", "p": "sp", "g": "sg"}
+
+
+def op(P, q, fn, out, *args, **kw):
+    views = [a for a in args if is_view(a)] + [a for a in kw.values() if is_view(a)]
+    reads = regions(views)
+    writes = []
+    if out[0] == "I":
+        writes += regions([out[1]])
+        reads += regions([out[2]])
+    else:
+        writes += regions([out])
+    sync_for(P, q, reads, writes)
+    sem = SEM_OF[q]
+    P["cnt"][sem] += 1
+    rargs = [resolve(P, a) if is_view(a) else a for a in args]
+    rkw = {k: (resolve(P, a) if is_view(a) else a) for k, a in kw.items()}
+    fn(resolve(P, out), *rargs, **rkw).then_inc(P["T"].sem[sem], 1)
+    note(P, q, reads, writes, sem, P["cnt"][sem])
+
+
+def rank_program(g, core, T, topo):
+    me = T.rank_of(core)
+    if me is None:
+        return
+    P = Plan().setup(g, T)
+    v, s, pe, y = g.vector, g.scalar, g.tensor, g.sync
+
+    def cp(out, in_): op(P, "v", v.tensor_copy, out, in_)
+    def tt(out, a, b, o): op(P, "v", v.tensor_tensor, out, a, b, o)
+    def ts(out, a, s1, o1, s2=None, o2=None):
+        if o2 is None:
+            op(P, "v", v.tensor_scalar, out, a, s1, None, o1)
+        else:
+            op(P, "v", v.tensor_scalar, out, a, s1, s2, o1, o2)
+    def scan(out, d0, d1): op(P, "v", v.tensor_tensor_scan, out, d0, d1, 0.0, O.mult, O.add)
+    def fill(out, c): op(P, "v", v.memset, out, c)
+    def act(out, in_, f, **kw): op(P, "s", s.activation, out, in_, f, **kw)
+    def mm(out, l, r, st, sp): op(P, "p", pe.matmul, out, l, r, st, sp)
+
+    def load(q, out, src, sem):
+        P["eng"][q].dma_start(resolve(P, out), src).then_inc(T.sem[sem], 16)
+        note(P, "d" + sem, [], regions([out]), sem, 16)
+    load("y", A("wkb", 0, 256, 1, 0, 8), T.wk[:], "dwk")
+    load("s", A("vt", 0, 1024), T.vp[:], "dvp")
+    load("y", A("quS", 0, 1024), T.qu[:], "dqu")
+    load("y", A("at", 0, 3200), T.am[:], "dam")
+    for j in range(16):
+        y.dma_start(T.pt[j:128:16, :], T.pay[:]).then_inc(T.sem["dpay"], 16)
+    note(P, "dpay", [], [("pt", 0, 3200, 1)], "dpay", 256)
+
+    op(P, "g", g.iota, A("pci", 0, 1), [[1, 1]], 0, 1)
+    op(P, "g", g.iota, A("mi", 0, 256), [[1, 256]], 0, 0)
+    op(P, "g", g.iota, A("l16", 0, 16), [[16, 16]], 0, 0)
+    def C(k): return A("col", k, k + 1)
+    p0 = A("pci", 0, 1)
+    ts(A("pci", 1, 2), p0, 15, O.bitwise_and)
+    ts(A("pci", 2, 3), p0, 4, O.arith_shift_right)
+    ts(A("pci", 3, 4), p0, 7, O.bitwise_and)
+    ts(A("pci", 4, 5), p0, 3, O.arith_shift_right, 1, O.bitwise_and)
+    cp(A("col", 0, 5), A("pci", 0, 5))
+    PF, PM, PG, P7, PH = C(0), C(1), C(2), C(3), C(4)
+    NEG, ADD1, NONEC, J256 = C(5), C(6), C(7), C(8)
+    mi = A("mi", 0, 256)
+    ts(A("l4", 0, 256), mi, 4, O.arith_shift_right)
+    ts(A("l15", 0, 256), mi, 15, O.bitwise_and)
+    l4h = A("l4", 0, 128)
+    ts(A("sel8", 0, 128, 1, 0, 8), A("l4", 0, 128, 1, 0, 8), A("col", 0, 1, 1, 0, 8), O.is_equal)
+    maskP, SC = A("b2", 0, 256), A("b2", 256, 512)
+    ts(maskP, A("l15", 0, 256), PM, O.is_equal)
+    ts(A("rst", 0, 256), A("l15", 0, 256), 0.0, O.not_equal)
+    ts(A("bs1", 0, 8), A("mi", 0, 8), PG, O.is_equal)
+    ts(NEG, PM, -4096.0, O.mult, -1.0, O.add)
+    ts(ADD1, PM, 4096.0, O.mult, 1.0, O.add)
+    ts(NONEC, PM, 4096.0, O.mult, float(NONE1), O.add)
+    ts(A("ut", 1024, 1032), A("mi", 0, 8), 0.0, O.mult, NONEC, O.add)
+    fill(A("vt", 1024, 1040), 0.0)
+    for a in list(range(7)) + list(range(8, 15)):
+        fill(A("eqx", 256 * a + (0 if a < 7 else 128), 256 * a + 16 * (a + 1)), 0.0)
+
+    def late_constants():
+        ts(A("idF", 0, 128), A("mi", 0, 128), PF, O.is_equal)
+        ts(A("bs64", 0, 8), A("mi", 0, 8), PG, O.is_equal, 65536.0, O.mult)
+        cp(A("idB", 0, 128), A("idF", 0, 128))
+        cp(A("maskS", 0, 256), maskP)
+        fill(A("ones", 0, 256), 1.0)
+        ts(A("blk1", 0, 128), l4h, PG, O.is_equal)
+        ts(A("blk8", 0, 128), l4h, PG, O.is_equal, 8.0, O.mult)
+        ts(J256, PM, 256.0, O.mult)
+        ts(A("woff", 0, 128), l4h, PG, O.is_equal, J256, O.mult)
+        ts(C(9), PG, 0.0, O.is_equal, 4096.0, O.mult)
+        ts(C(10), PG, 1.0, O.is_equal, 64.0, O.mult)
+        ts(C(11), PG, 2.0, O.is_equal)
+        ts(C(14), PG, 3.0, O.is_equal)
+        tt(C(12), C(10), C(11), O.add)
+        tt(C(13), C(12), C(9), O.add)
+        ts(A("col", 18, 21), A("col", 12, 15), PH, O.mult)
+        tt(A("col", 15, 18), A("col", 12, 15), A("col", 18, 21), O.subtract)
+        for k in range(3):
+            for h in range(2):
+                w = 15 + 3 * h + k
+                ts(A("selx", 128 * (2 * k + h), 128 * (2 * k + h) + 128, 1, 0, 64), A("l4", 0, 128, 1, 0, 64),
+                   A("col", 3, 4, 1, 0, 64), O.is_equal, A("col", w, w + 1, 1, 0, 64), O.mult)
+        ts(A("dumpB", 0, 16), A("l16", 0, 16), PM, O.add, 1025.0, O.add)
+        ts(A("dumpA", 0, 16), A("l16", 0, 16), PM, O.add, 3200.0, O.add)
+        prefill(0)
+
+    def prefill(k):
+        for r in range(8):
+            fill(A("win%d" % k, 256 * r + 1, 256 * r + 33), float(1024 * r + 1025))
+
+    def pair_ops(sc, sbase, u16, x, half_pairs):
+        tt(A("eqd", 0, 256), A(sc, sbase, sbase + 256), x, O.is_equal)
+        for a in range(15):
+            c = sbase + 16 * a + 15
+            ts(A("eqx", 256 * a + 16 * (a + 1), 256 * a + 256), A(u16, 16 * (a + 1), 256), A(sc, c, c + 1), O.is_equal)
+
+    for st in range(3):
+        last = st == 2
+        if st == 0:
+            ts(A("wkf", 0, 256, 1, 0, 8), A("wkb", 0, 256, 1, 0, 8), 1.0, O.add)
+            mm(A("b4", 256, 512), A("sel8", 0, 128, 1, 0, 8), A("wkf", 0, 256, 1, 0, 8), True, True)
+            cp(A("xz", 0, 256), A("b4", 256, 512))
+            x, base = A("xz", 0, 256), 1
+        else:
+            cp(A("ci", 0, 256), A("land%d" % (st - 1), 0, 256))
+            ts(A("xi", 0, 256), A("ci", 0, 256), 16383, O.bitwise_and)
+            x, base = A("xi", 0, 256), 1 + 1024 * me
+        tt(A("M1", 0, 256), x, maskP, O.mult)
+        scan(SC, A("rst", 0, 256), A("M1", 0, 256))
+        scW = A("b2", 256 + 15, 512, 16)
+        ts(A("BWu", 0, 16), scW, float(-base), O.add)
+        BW = A("BWu", 0, 16)
+
+        def dedup1():
+            cp(A("xu", 0, 256), x)
+            pair_ops("b2", 256, "xu", x, True)
+
+        def dedup1_count():
+            for h in range(2):
+                out = A("b4", 16 + 8 * h, 24 + 8 * h)
+                mm(out, A("eqd", 128 * h, 128 * h + 128), A("bs1", 0, 8), True, False)
+                last_a = 7 if h == 0 else 15
+                for a in range(last_a):
+                    mm(out, A("eqx", 256 * a + 128 * h, 256 * a + 128 * h + 128), A("bs1", 0, 8), False, a == last_a - 1)
+
+        if st == 0:
+            dedup1()
+            late_constants()
+            cp(A("V2", 0, 256), IND(A("vt", 0, 1040), BW))
+            ts(A("ut", 0, 1024), A("quS", 0, 1024), ADD1, O.add)
+        else:
+            ts(A("cI", 0, 256), A("ci", 0, 256), 14, O.arith_shift_right)
+            tt(A("V1", 0, 256), IND(A("vt", 0, 1040), BW), A("cI", 0, 256), O.subtract)
+            ts(A("V2", 0, 256), A("V1", 0, 256), -255.0, O.max)
+        act(A("UI", 0, 256), IND(A("ut", 0, 1032), BW), F.Copy)
+        for i in range(16):
+            act(A("NVx", i, 2048, 16), A("V2", 0, 128), F.Copy, scale=-1.0)
+        ts(A("Uo", 0, 256), IND(A("ut", 0, 1032), BW), NEG, O.add)
+        ts(A("neg", 0, 256), A("V2", 0, 256), 0.0, O.is_lt)
+        if st != 0:
+            dedup1()
+        NVP = A("b3", 0, 256)
+        act(NVP, A("V2", 0, 256), F.Copy, scale=-1.0)
+        for c in range(2):
+            act(A("Ag", 1024 * c, 1024 * c + 1024), IND(A("at", 0, 3200), A("Uo", 128 + 64 * c, 192 + 64 * c)), F.Copy)
+        act(A("NVr", 0, 256), A("V2", 0, 256), F.Relu, scale=-1.0)
+        for h in range(2):
+            mm(A("b%d" % h, 0, 128), A("UI", 128 * h, 128 * h + 128), A("idF", 0, 128), True, False)
+        for h in range(2):
+            mm(A("b4", 8 * h, 8 * h + 8), A("neg", 128 * h, 128 * h + 128), A("bs1", 0, 8), True, True)
+        dedup1_count()
+        tt(A("ge0", 0, 2048), IND(A("at", 0, 3200), A("Uo", 0, 128)), A("NVx", 0, 2048), O.is_ge)
+        for i in range(16):
+            mm(A("b0", i, 128, 16), A("ge0", i, 2048, 16), A("bs64", 0, 8), False, i == 15)
+        act(A("so", 0, 64), A("b0", 1, 128, 2), F.Copy)
+        ts(A("sm", 0, 16), A("b4", 0, 16), 0.0, O.is_equal, float(XKEY), O.mult)
+        ts(A("sm", 16, 32), A("b4", 16, 32), 1.5, O.is_gt, float(XKEY), O.mult)
+        ts(A("digB", 48, 64), A("b4", 16, 32), 1.5, O.is_gt)
+        for i in range(16):
+            tt(A("ge1", 128 * i, 128 * i + 128), A("Ag", i, 2048, 16), A("b3", 128, 256), O.is_ge)
+            mm(A("b1", i, 128, 16), A("ge1", 128 * i, 128 * i + 128), A("bs64", 0, 8), False, i == 15)
+        act(A("so", 64, 128), A("b1", 1, 128, 2), F.Copy)
+        tt(A("sm", 32, 48), A("sm", 0, 16), A("sm", 16, 32), O.max)
+        tt(A("m1", 0, 64), A("b0", 0, 128, 2), A("so", 0, 64), O.max)
+        tt(A("m1", 64, 128), A("b1", 0, 128, 2), A("so", 64, 128), O.max)
+        tt(A("m2", 0, 64), A("m1", 0, 128, 2), A("m1", 1, 128, 2), O.max)
+        tt(A("m3", 0, 32), A("m2", 0, 64, 2), A("m2", 1, 64, 2), O.max)
+        tt(A("m4", 0, 16), A("m3", 0, 32, 2), A("m3", 1, 32, 2), O.max)
+        tt(A("ki", 0, 16), A("m4", 0, 16), A("sm", 32, 48), O.max)
+        ki = A("ki", 0, 16)
+        ts(A("digI", 16, 32), ki, 6, O.arith_shift_right, 63, O.bitwise_and)
+        ts(A("digI", 32, 48), ki, 63, O.bitwise_and)
+        ts(A("digI", 0, 16), ki, 12, O.arith_shift_right, 15, O.bitwise_and)
+        cp(A("digB", 0, 48), A("digI", 0, 48))
+        mm(A("b4", 128, 256, 1, 0, 64), A("digB", 0, 64), A("idB", 0, 128), True, True)
+        act(A("TTs", 0, 128, 1, 0, 64), A("b4", 128, 256, 1, 0, 64), F.Copy)
+        for k, (bank, c0) in enumerate((("b5", 0), ("b6", 0), ("b6", 256))):
+            for h in range(2):
+                mm(A(bank, c0 + 128 * h, c0 + 128 * h + 128), A("selx", 128 * (2 * k + h), 128 * (2 * k + h) + 128, 1, 0, 64),
+                   A("TTs", 0, 128, 1, 0, 64), True, True)
+        RL = A("b5", 0, 256)
+        tt(A("M5", 0, 256), RL, A("maskS", 0, 256), O.mult)
+        cp(A("Lu", 0, 256), RL)
+        scan(A("SC5", 0, 256), A("rst", 0, 256), A("M5", 0, 256))
+        l5 = A("SC5", 15, 256, 16)
+        pair_ops("SC5", 0, "Lu", RL, False)
+        ts(A("LWu", 0, 16), l5, -1.0, O.add)
+        LW = A("LWu", 0, 16)
+        CN = A("b7", 0, 256)
+        mm(CN, A("blk8", 0, 128), A("eqd", 0, 256), True, False)
+        for a in range(15):
+            mm(A("b7", 16 * (a + 1), 256), A("blk8", 0, 128), A("eqx", 256 * a + 16 * (a + 1), 256 * a + 256), False, a == 14)
+        if st == 0:
+            fill(A("pt", 3199, 3200), 8192)
+        cp(A("payf", 0, 256), IND(A("pt", 0, 3200), LW))
+        tt(A("tt", 0, 256), IND(A("at", 0, 3200), LW), A("NVr", 0, 256), O.min)
+        ts(A("r8", 0, 256), A("payf", 0, 256), 1.0 / 1024, O.mult, -511.5 / 1024 - 8.0, O.add)
+        act(A("t16", 0, 256), A("tt", 0, 256), F.Identity, bias=1.0, scale=16384.0)
+        if not last:
+            act(A("Agl", 0, 256), IND(A("at", 0, 3200), LW), F.Copy)
+        tt(A("zz", 0, 256), CN, A("r8", 0, 256), O.add)
+        OH, cum = A("OH", 0, 256), A("b3", 256, 512)
+        ts(OH, A("zz", 0, 256), 8.0, O.min, PM, O.is_equal)
+        scan(cum, A("ones", 0, 256), OH)
+        OFF = A("b5", 256, 512)
+        mm(OFF, A("woff", 0, 128), OH, True, False)
+        tt(A("prod", 0, 256), cum, OH, O.mult)
+        mm(OFF, A("blk1", 0, 128), A("prod", 0, 256), False, True)
+        tt(A("M6", 0, 256), OFF, A("maskS", 0, 256), O.mult)
+        scan(A("SC6", 0, 256), A("rst", 0, 256), A("M6", 0, 256))
+        o6 = A("SC6", 15, 256, 16)
+        cp(A("OWu", 0, 16), o6)
+        win, land = "win%d" % st, "land%d" % st
+        tt(IND(A(win, 0, WIN), A("OWu", 0, 16)), A("t16", 0, 256), A("payf", 0, 256), O.add)
+        sync_for(P, "g", [(win, 0, WIN, 1)], [])
+        mk = masks(topo, T.cores, me)
+        transfers = []
+        for k in range(1, 8):
+            r = (me + k) % 8
+            rid, pid = topo.addr(T.cores[r], core)
+            transfers.append(RemoteDMATransfer(dst_ids=[DstId(rid=rid, pnc=pid)], dma_engine_mask=sum(1 << e for e in mk[r]),
+                                               remote_sem=T.sem["arr%d" % st], src=T[win][:, 256 * r + 1:256 * r + 33],
+                                               dst=T[land][:, 32 * me:32 * me + 32]))
+        g.remote_dma_fused(transfers, local_sem=T.sem["loc"])
+        note(P, "g", [(win, 0, WIN, 1)], [], "loc", (st + 1) * sum(len(mk[r]) for r in mk))
+        arrive = sum(len(masks(topo, T.cores, q)[me]) for q in range(8) if q != me)
+        for q in range(8):
+            if q != me:
+                note(P, "remote", [], [(land, 32 * q, 32 * q + 32, 1)], "arr%d" % st, arrive)
+        cp(A(land, 32 * me, 32 * me + 32), A(win, 256 * me + 1, 256 * me + 33))
+        okP = A("b3", 256, 512)
+        ts(okP, CN, 8.0, O.is_equal)
+        RD = A("b6", 256, 512)
+        tt(A("M7", 0, 256), RD, A("maskS", 0, 256), O.mult)
+        tt(A("tm", 0, 256), okP, A("tt", 0, 256), O.mult)
+        scan(A("SC7", 0, 256), A("rst", 0, 256), A("M7", 0, 256))
+        tt(A("Vn", 0, 256), A("tm", 0, 256), NVP, O.subtract)
+        tt(A("sm", 48, 64), A("SC7", 15, 256, 16), A("dumpB", 0, 16), O.mult)
+        ts(A("sm", 64, 80), scW, float(-base), O.add)
+        tt(A("sm", 80, 96), A("sm", 48, 64), A("sm", 64, 80), O.max)
+        cp(A("boU", 0, 16), A("sm", 80, 96))
+        cp(IND(A("vt", 0, 1296), A("boU", 0, 16)), A("Vn", 0, 256))
+        if last:
+            break
+        okX = A("b7", 256, 512)
+        ts(okX, CN, 8.0, O.is_equal, NONEC, O.mult)
+        tt(A("OHu", 0, 256), A("b6", 0, 256), A("UI", 0, 256), O.is_equal)
+        ts(A("sm", 96, 112), o6, 2048.5, O.is_gt)
+        tt(A("OHk", 0, 256), okX, A("OHu", 0, 256), O.mult)
+        ts(A("sm", 112, 128), l5, -1.0, O.add)
+        tt(A("UIn", 0, 256), A("UI", 0, 256), A("OHk", 0, 256), O.max)
+        tt(A("sm", 96, 112), A("sm", 96, 112), A("dumpA", 0, 16), O.mult)
+        tt(A("An", 0, 256), A("Agl", 0, 256), A("tm", 0, 256), O.subtract)
+        tt(A("sm", 96, 112), A("sm", 96, 112), A("sm", 112, 128), O.max)
+        cp(IND(A("ut", 0, 1296), A("boU", 0, 16)), A("UIn", 0, 256))
+        cp(A("aoU", 0, 16), A("sm", 96, 112))
+        cp(IND(A("at", 0, 3456), A("aoU", 0, 16)), A("An", 0, 256))
+        prefill(st + 1)
+
+    def store(q, dst, src_view, sem):
+        sync_for(P, q, regions([src_view]), [])
+        P["eng"][q].dma_start(dst, resolve(P, src_view)).then_inc(T.sem[sem], 16)
+    store("y", T.yv[:], A("vt", 0, 1024), "dyv")
+    cp(A("ci", 0, 256), A("land2", 0, 256))
+    ts(A("xi", 0, 256), A("ci", 0, 256), 16383, O.bitwise_and)
+    ts(A("cI", 0, 256), A("ci", 0, 256), 14, O.arith_shift_right)
+    ts(A("ywS", 0, 256), A("xi", 0, 256), float(-(1 + 1024 * me)), O.add)
+    store("y", T.yw[:], A("ywS", 0, 256, 1, 0, 128)[:5] + ((0, 128)) if False else A("ywS", 0, 256), "dyw") if False else None
+    sync_for(P, "y", regions([A("ywS", 0, 256)]), [])
+    y.dma_start(T.yw[:], T.ywS[0:128:16, 0:256]).then_inc(T.sem["dyw"], 16)
+    cp(A("ycS", 0, 256), A("cI", 0, 256))
+    store("s", T.yc[:], A("ycS", 0, 256), "dyc")
+    for sem in ("sv", "ss", "sp", "sg"):
+        g.wait_ge(T.sem[sem], P["cnt"][sem])
+    for sem in ("dwk", "dvp", "dqu", "dam", "dyv", "dyw", "dyc"):
+        g.wait_ge(T.sem[sem], 16)
+    g.wait_ge(T.sem["dpay"], 256)
+    g.wait_ge(T.sem["loc"], 3 * sum(len(mk[r]) for r in mk))
+    for k in range(3):
+        g.wait_ge(T.sem["arr%d" % k], arrive)
+
+
+def masks(topo, cores, q):
+    src = cores[q]
+    others = [r for r in range(len(cores)) if r != q]
+    near = [r for r in others if cores[r] in topo.cores_of(src)]
+    far = [r for r in others if r not in near]
+    free = list(topo.engines(src, cores[far[0]]))
+    out = {}
+    for r in far:
+        e = [x for x in free if x in topo.engines(src, cores[r])][0]
+        out[r] = [e]
+        free.remove(e)
+    for n, r in enumerate(near):
+        k = len(free) // (len(near) - n)
+        while k & (k - 1):
+            k -= 1
+        out[r] = free[:k]
+        free = free[k:]
+    return out

@@ -2,48 +2,55 @@ from concourse.bass import DstId, RemoteDMATransfer
 from concourse.mybir import AluOpType as O, ActivationFunctionType as F
 
 WIN = 2312
-SCRATCH = {
-    "wkb": ("sbuf", [128, 256], "int32"), "wkf": ("sbuf", [128, 256], "float32"), "xz": ("sbuf", [128, 256], "float32"),
-    "quS": ("sbuf", [128, 1024], "int32"), "ut": ("sbuf", [128, 1296], "float32"), "vt": ("sbuf", [128, 1296], "bfloat16"),
-    "at": ("sbuf", [128, 3456], "bfloat16"), "pt": ("sbuf", [128, 3200], "int32"),
-    "mi": ("sbuf", [128, 256], "int32"), "l4": ("sbuf", [128, 256], "int32"), "l15": ("sbuf", [128, 256], "int32"),
-    "pci": ("sbuf", [128, 8], "int32"), "col": ("sbuf", [128, 32], "float32"), "l16": ("sbuf", [128, 16], "int32"),
-    "dumpA": ("sbuf", [128, 16], "float32"), "dumpB": ("sbuf", [128, 16], "float32"),
-    "maskS": ("sbuf", [128, 256], "bfloat16"), "rst": ("sbuf", [128, 256], "bfloat16"), "ones": ("sbuf", [128, 256], "bfloat16"),
-    "blk1": ("sbuf", [128, 128], "bfloat16"), "blk8": ("sbuf", [128, 128], "bfloat16"), "woff": ("sbuf", [128, 128], "bfloat16"),
-    "bs1": ("sbuf", [128, 8], "bfloat16"), "bs64": ("sbuf", [128, 8], "bfloat16"),
-    "idF": ("sbuf", [128, 128], "float32"), "idB": ("sbuf", [128, 128], "bfloat16"), "sel8": ("sbuf", [128, 128], "float32"),
-    "selx": ("sbuf", [128, 768], "bfloat16"),
-    "ci": ("sbuf", [128, 256], "int32"), "xi": ("sbuf", [128, 256], "int32"), "cI": ("sbuf", [128, 256], "int32"),
-    "M1": ("sbuf", [128, 256], "float32"), "M5": ("sbuf", [128, 256], "float32"), "M6": ("sbuf", [128, 256], "float32"), "M7": ("sbuf", [128, 256], "float32"),
-    "SC5": ("sbuf", [128, 256], "float32"), "SC6": ("sbuf", [128, 256], "float32"), "SC7": ("sbuf", [128, 256], "float32"),
-    "BWu": ("sbuf", [128, 16], "uint16"), "LWu": ("sbuf", [128, 16], "uint16"), "OWu": ("sbuf", [128, 16], "uint16"),
-    "boU": ("sbuf", [128, 16], "uint16"), "aoU": ("sbuf", [128, 16], "uint16"), "sm": ("sbuf", [128, 128], "float32"),
-    "xu": ("sbuf", [128, 256], "uint16"), "Lu": ("sbuf", [128, 256], "uint16"), "Uo": ("sbuf", [128, 256], "uint16"),
-    "UI": ("sbuf", [128, 256], "float32"), "V1": ("sbuf", [128, 256], "bfloat16"), "V2": ("sbuf", [128, 256], "bfloat16"),
-    "neg": ("sbuf", [128, 256], "bfloat16"), "NVr": ("sbuf", [128, 256], "bfloat16"), "NVx": ("sbuf", [128, 2048], "bfloat16"),
-    "eqx": ("sbuf", [128, 3840], "bfloat16"), "eqd": ("sbuf", [128, 256], "bfloat16"),
-    "ge0": ("sbuf", [128, 2048], "bfloat16"), "Ag": ("sbuf", [128, 2048], "bfloat16"), "ge1": ("sbuf", [128, 2048], "bfloat16"),
-    "so": ("sbuf", [128, 128], "float32"), "m1": ("sbuf", [128, 128], "float32"), "m2": ("sbuf", [128, 64], "float32"),
-    "m3": ("sbuf", [128, 32], "float32"), "m4": ("sbuf", [128, 16], "float32"),
-    "ki": ("sbuf", [128, 16], "int32"), "digI": ("sbuf", [128, 48], "int32"), "digB": ("sbuf", [128, 64], "bfloat16"),
-    "TTs": ("sbuf", [128, 128], "bfloat16"),
-    "tt": ("sbuf", [128, 256], "bfloat16"), "t16": ("sbuf", [128, 256], "float32"), "Agl": ("sbuf", [128, 256], "bfloat16"),
-    "payf": ("sbuf", [128, 256], "float32"), "r8": ("sbuf", [128, 256], "int32"), "zz": ("sbuf", [128, 256], "bfloat16"),
-    "OH": ("sbuf", [128, 256], "bfloat16"), "prod": ("sbuf", [128, 256], "bfloat16"),
-    "tm": ("sbuf", [128, 256], "bfloat16"), "Vn": ("sbuf", [128, 256], "bfloat16"), "An": ("sbuf", [128, 256], "bfloat16"),
-    "OHu": ("sbuf", [128, 256], "float32"), "OHk": ("sbuf", [128, 256], "float32"), "UIn": ("sbuf", [128, 256], "float32"),
-    "ycS": ("sbuf", [128, 256], "bfloat16"), "ywS": ("sbuf", [128, 256], "float32"),
-}
-for _s in range(3):
-    SCRATCH["win%d" % _s] = ("sbuf", [128, WIN], "float32")
-    SCRATCH["land%d" % _s] = ("sbuf", [128, 256], "float32")
-for _s in range(8):
-    SCRATCH["b%d" % _s] = ("psum", [128, 512], "float32")
+SCRATCH = {}
+for _n in "wkb ci xi r8".split():
+    SCRATCH[_n] = ("sbuf", [128, 256], "int32")
+for _n in "wkf xz UI M1 M5 M6 SC5 SC6 t16 payf OHu UIn ywS cm land0 land1 land2".split():
+    SCRATCH[_n] = ("sbuf", [128, 256], "float32")
+for _n in "maskS rst ones V1 V2 NVr eqd eqe tt zz OH prod Vn An Agl cB".split():
+    SCRATCH[_n] = ("sbuf", [128, 256], "bfloat16")
+for _n in "blk1 blkT blk8 woff idB selb selL selC TTs0 TTs1".split():
+    SCRATCH[_n] = ("sbuf", [128, 128], "bfloat16")
+for _n in "BWu LWu OWu boU aoU".split():
+    SCRATCH[_n] = ("sbuf", [128, 16], "uint16")
+for _n in "xu Lu Uo".split():
+    SCRATCH[_n] = ("sbuf", [128, 256], "uint16")
+for _n in "NVx ge0 Ag ge1".split():
+    SCRATCH[_n] = ("sbuf", [128, 2048], "bfloat16")
+for _n in "onesF idF sel8 selT".split():
+    SCRATCH[_n] = ("sbuf", [128, 128], "float32")
+for _n in range(3):
+    SCRATCH["win%d" % _n] = ("sbuf", [128, WIN], "float32")
+for _n in range(8):
+    SCRATCH["b%d" % _n] = ("psum", [128, 512], "float32")
+for _n in range(2):
+    SCRATCH["so%d" % _n] = ("sbuf", [128, 64], "float32")
+    SCRATCH["mx%d" % _n] = ("sbuf", [128, 128], "float32")
+    SCRATCH["ki%d" % _n] = ("sbuf", [128, 8], "int32")
+    SCRATCH["digI%d" % _n] = ("sbuf", [128, 24], "int32")
+    SCRATCH["digB%d" % _n] = ("sbuf", [128, 32], "bfloat16")
+SCRATCH["quS"] = ("sbuf", [128, 1032], "int32")
+SCRATCH["ut"] = ("sbuf", [128, 1296], "float32")
+SCRATCH["vt"] = ("sbuf", [128, 1296], "bfloat16")
+SCRATCH["at"] = ("sbuf", [128, 3456], "bfloat16")
+SCRATCH["pt"] = ("sbuf", [128, 3200], "int32")
+SCRATCH["eqx"] = ("sbuf", [128, 3840], "bfloat16")
+SCRATCH["l15"] = ("sbuf", [128, 256], "int32")
+SCRATCH["l4"] = ("sbuf", [128, 128], "int32")
+SCRATCH["l16"] = ("sbuf", [128, 16], "int32")
+SCRATCH["pci"] = ("sbuf", [128, 8], "int32")
+SCRATCH["col"] = ("sbuf", [128, 32], "float32")
+SCRATCH["bs64"] = ("sbuf", [128, 8], "bfloat16")
+SCRATCH["dumpA"] = ("sbuf", [128, 16], "float32")
+SCRATCH["dumpB"] = ("sbuf", [128, 16], "float32")
+SCRATCH["sm"] = ("sbuf", [128, 192], "float32")
 SEMAPHORES = ["sv", "ss", "sp", "sg", "dwk", "dvp", "dqu", "dam", "dpay", "dyv", "dyw", "dyc", "loc", "arr0", "arr1", "arr2"]
 NONE1 = 3200
 XKEY = 272 * 4096 + NONE1
-BIGW = WIN
+LOW = 2097152
+MAGIC = 12582912.0
+XL = 224
+NV = 4
 
 
 def A(name, c0, c1, step=1, p0=0, p1=128):
@@ -58,18 +65,10 @@ def is_view(x):
     return isinstance(x, tuple) and len(x) > 0 and (x[0] == "A" or x[0] == "I")
 
 
-class Plan:
-    def setup(self, g, T):
-        return {"g": g, "T": T, "hist": {}, "known": {q: {} for q in "vspyg"}, "cnt": {"sv": 0, "ss": 0, "sp": 0, "sg": 0},
-                "eng": {"v": g.vector, "s": g.scalar, "p": g.tensor, "y": g.sync, "g": g}}
-
-
 def hits(a, b):
     if a[2] <= b[1] or b[2] <= a[1]:
         return False
-    if a[3] > 1 and a[3] == b[3] and (a[1] - b[1]) % a[3] != 0:
-        return False
-    return True
+    return not (a[3] > 1 and a[3] == b[3] and (a[1] - b[1]) % a[3] != 0)
 
 
 def is_psum(name):
@@ -100,19 +99,10 @@ def sync_for(P, q, reads, writes):
     for kind, regs in (("r", reads), ("w", writes)):
         for r in regs:
             ps = is_psum(r[0])
-            for h in P["hist"].get(r[0], []):
-                hk, hr, hq, sem, val, clock = h
+            for hk, hr, hq, sem, val, clock in P["hist"].get(r[0], []):
                 same = hq == q
-                if ps and not same:
-                    pass
-                else:
-                    if kind == "r" and hk == "r":
-                        continue
-                    if same and (kind == "w" and hk == "r"):
-                        continue
-                    if same and kind == "w" and q == "p":
-                        continue
-                    if not hits(r, hr):
+                if same or not ps:
+                    if (hk == "r" and (kind == "r" or same)) or (same and kind == "w" and q == "p") or not hits(r, hr):
                         continue
                 need.append((sem, val, clock))
     best = {}
@@ -120,8 +110,7 @@ def sync_for(P, q, reads, writes):
         if P["known"][q].get(sem, 0) < val and (sem not in best or best[sem][0] < val):
             best[sem] = (val, clock)
     for sem in list(best):
-        val = best[sem][0]
-        if any(s2 != sem and best[s2][1].get(sem, 0) >= val for s2 in best):
+        if any(s2 != sem and best[s2][1].get(sem, 0) >= best[sem][0] for s2 in best):
             del best[sem]
     for sem in best:
         val, clock = best[sem]
@@ -139,7 +128,7 @@ def note(P, q, reads, writes, sem, val):
         for r in regs:
             lst = P["hist"].setdefault(r[0], [])
             if kind == "w" and r[3] == 1:
-                lst[:] = [h for h in lst if not (r[1] <= h[1][1] and h[1][2] <= r[2] and (h[2] == q or h[0] == "r" or not is_psum(r[0])) and h[2] == q)]
+                lst[:] = [h for h in lst if not (h[2] == q and r[1] <= h[1][1] and h[1][2] <= r[2])]
             lst.append((kind, r, q, sem, val, clock))
 
 
@@ -147,29 +136,37 @@ SEM_OF = {"v": "sv", "s": "ss", "p": "sp", "g": "sg"}
 
 
 def op(P, q, fn, out, *args, **kw):
-    views = [a for a in args if is_view(a)] + [a for a in kw.values() if is_view(a)]
-    reads = regions(views)
-    writes = []
+    reads = regions([a for a in args if is_view(a)] + [a for a in kw.values() if is_view(a)])
     if out[0] == "I":
-        writes += regions([out[1]])
+        writes = regions([out[1]])
         reads += regions([out[2]])
     else:
-        writes += regions([out])
+        writes = regions([out])
     sync_for(P, q, reads, writes)
     sem = SEM_OF[q]
     P["cnt"][sem] += 1
-    rargs = [resolve(P, a) if is_view(a) else a for a in args]
-    rkw = {k: (resolve(P, a) if is_view(a) else a) for k, a in kw.items()}
-    fn(resolve(P, out), *rargs, **rkw).then_inc(P["T"].sem[sem], 1)
+    fn(resolve(P, out), *[resolve(P, a) if is_view(a) else a for a in args],
+       **{k: (resolve(P, a) if is_view(a) else a) for k, a in kw.items()}).then_inc(P["T"].sem[sem], 1)
     note(P, q, reads, writes, sem, P["cnt"][sem])
+
+
+def weave(first, second, start):
+    second = list(second)
+    for n, f in enumerate(first):
+        f()
+        if n >= start and second:
+            second.pop(0)()
+    for f in second:
+        f()
 
 
 def rank_program(g, core, T, topo):
     me = T.rank_of(core)
     if me is None:
         return
-    P = Plan().setup(g, T)
     v, s, pe, y = g.vector, g.scalar, g.tensor, g.sync
+    P = {"T": T, "hist": {}, "known": {q: {} for q in "vspyg"}, "cnt": {"sv": 0, "ss": 0, "sp": 0, "sg": 0},
+         "eng": {"v": v, "s": s, "p": pe, "y": y, "g": g}}
 
     def cp(out, in_): op(P, "v", v.tensor_copy, out, in_)
     def tt(out, a, b, o): op(P, "v", v.tensor_tensor, out, a, b, o)
@@ -178,10 +175,14 @@ def rank_program(g, core, T, topo):
             op(P, "v", v.tensor_scalar, out, a, s1, None, o1)
         else:
             op(P, "v", v.tensor_scalar, out, a, s1, s2, o1, o2)
-    def scan(out, d0, d1): op(P, "v", v.tensor_tensor_scan, out, d0, d1, 0.0, O.mult, O.add)
+    def scan(out, d0, d1, ini=0.0): op(P, "v", v.tensor_tensor_scan, out, d0, d1, ini, O.mult, O.add)
     def fill(out, c): op(P, "v", v.memset, out, c)
     def act(out, in_, f, **kw): op(P, "s", s.activation, out, in_, f, **kw)
     def mm(out, l, r, st, sp): op(P, "p", pe.matmul, out, l, r, st, sp)
+    def iota(out, pat, base, cm, **kw): op(P, "g", g.iota, out, pat, base, cm, **kw)
+    def pick(out, in_, pat, cmp, base, cm): op(P, "g", g.affine_select, out, in_, pat, cmp, 0.0, base, cm)
+    def H(name, h, c0=0): return A(name, c0 + 128 * h, c0 + 128 * h + 128)
+    def C(k, n=128): return A("col", k, k + 1, 1, 0, n)
 
     def load(q, out, src, sem):
         P["eng"][q].dma_start(resolve(P, out), src).then_inc(T.sem[sem], 16)
@@ -194,273 +195,318 @@ def rank_program(g, core, T, topo):
         y.dma_start(T.pt[j:128:16, :], T.pay[:]).then_inc(T.sem["dpay"], 16)
     note(P, "dpay", [], [("pt", 0, 3200, 1)], "dpay", 256)
 
-    op(P, "g", g.iota, A("pci", 0, 1), [[1, 1]], 0, 1)
-    op(P, "g", g.iota, A("mi", 0, 256), [[1, 256]], 0, 0)
-    op(P, "g", g.iota, A("l16", 0, 16), [[16, 16]], 0, 0)
-    def C(k): return A("col", k, k + 1)
+    imp = {"allow_small_or_imprecise_dtypes": True}
+    iota(A("pci", 0, 1), [[1, 1]], 0, 1)
+    iota(A("l15", 0, 256), [[0, 16], [1, 16]], 0, 0)
+    iota(A("onesF", 0, 128), [[0, 128]], 1, 0, **imp)
+    pick(A("selT", 0, 128, 1, 0, 8), A("onesF", 0, 128, 1, 0, 8), [[1, 128]], O.is_ge, 0, -16)
+    pick(A("sel8", 0, 128, 1, 0, 8), A("selT", 0, 128, 1, 0, 8), [[-1, 128]], O.is_ge, 15, 16)
+    iota(A("ones", 0, 256), [[0, 256]], 1, 0, **imp)
+    pick(A("blkT", 0, 128), A("ones", 0, 128), [[-16, 8], [0, 16]], O.is_ge, 0, 1)
+    pick(A("blk1", 0, 128), A("blkT", 0, 128), [[16, 8], [0, 16]], O.is_ge, 15, -1)
+    pick(A("idF", 0, 128), A("onesF", 0, 128), [[-1, 128]], O.is_equal, 0, 1)
+    pick(A("idB", 0, 128), A("ones", 0, 128), [[-1, 128]], O.is_equal, 0, 1)
+    iota(A("l4", 0, 128), [[1, 8], [0, 16]], 0, 0)
+    iota(A("l16", 0, 16), [[16, 16]], 0, 0)
+    for k in range(3):
+        for r in range(8):
+            iota(A("win%d" % k, 256 * r + 1, 256 * r + 33), [[0, 32]], 1024 * r + 1025 - 4096, 0, **imp)
     p0 = A("pci", 0, 1)
     ts(A("pci", 1, 2), p0, 15, O.bitwise_and)
-    ts(A("pci", 2, 3), p0, 4, O.arith_shift_right)
+    ts(A("pci", 2, 3), p0, 3, O.arith_shift_right)
     ts(A("pci", 3, 4), p0, 7, O.bitwise_and)
-    ts(A("pci", 4, 5), p0, 3, O.arith_shift_right, 1, O.bitwise_and)
-    cp(A("col", 0, 5), A("pci", 0, 5))
-    PF, PM, PG, P7, PH = C(0), C(1), C(2), C(3), C(4)
-    NEG, ADD1, NONEC, J256 = C(5), C(6), C(7), C(8)
-    mi = A("mi", 0, 256)
-    ts(A("l4", 0, 256), mi, 4, O.arith_shift_right)
-    ts(A("l15", 0, 256), mi, 15, O.bitwise_and)
-    l4h = A("l4", 0, 128)
-    ts(A("sel8", 0, 128, 1, 0, 8), A("l4", 0, 128, 1, 0, 8), A("col", 0, 1, 1, 0, 8), O.is_equal)
-    maskP, SC = A("b2", 0, 256), A("b2", 256, 512)
-    ts(maskP, A("l15", 0, 256), PM, O.is_equal)
+    cp(A("col", 0, 4), A("pci", 0, 4))
+    PM, PD = C(1), C(2)
+    ADD1, NONEC, NNEG, N9, J256, NEG = C(4), C(5), C(6), C(7), C(8), C(9)
+    maskP = lambda h: H("b2", h)
+    SC = lambda h: H("b2", h, 256)
+    ts(A("b2", 0, 256), A("l15", 0, 256), PM, O.is_equal)
     ts(A("rst", 0, 256), A("l15", 0, 256), 0.0, O.not_equal)
-    ts(A("bs1", 0, 8), A("mi", 0, 8), PG, O.is_equal)
     ts(NEG, PM, -4096.0, O.mult, -1.0, O.add)
     ts(ADD1, PM, 4096.0, O.mult, 1.0, O.add)
     ts(NONEC, PM, 4096.0, O.mult, float(NONE1), O.add)
-    ts(A("ut", 1024, 1032), A("mi", 0, 8), 0.0, O.mult, NONEC, O.add)
+    ts(A("ut", 1024, 1032), A("l15", 0, 8), 0.0, O.mult, NONEC, O.add)
+    fill(A("quS", 1024, 1032), NONE1 - 1)
     fill(A("vt", 1024, 1040), 0.0)
     for a in list(range(7)) + list(range(8, 15)):
         fill(A("eqx", 256 * a + (0 if a < 7 else 128), 256 * a + 16 * (a + 1)), 0.0)
+    blksel = A("blk1", 0, 128, 16)
 
     def late_constants():
-        ts(A("idF", 0, 128), A("mi", 0, 128), PF, O.is_equal)
-        ts(A("bs64", 0, 8), A("mi", 0, 8), PG, O.is_equal, 65536.0, O.mult)
-        cp(A("idB", 0, 128), A("idF", 0, 128))
-        cp(A("maskS", 0, 256), maskP)
-        fill(A("ones", 0, 256), 1.0)
-        ts(A("blk1", 0, 128), l4h, PG, O.is_equal)
-        ts(A("blk8", 0, 128), l4h, PG, O.is_equal, 8.0, O.mult)
+        ts(A("maskS", 0, 256), A("l15", 0, 256), PM, O.is_equal)
         ts(J256, PM, 256.0, O.mult)
-        ts(A("woff", 0, 128), l4h, PG, O.is_equal, J256, O.mult)
-        ts(C(9), PG, 0.0, O.is_equal, 4096.0, O.mult)
-        ts(C(10), PG, 1.0, O.is_equal, 64.0, O.mult)
-        ts(C(11), PG, 2.0, O.is_equal)
-        ts(C(14), PG, 3.0, O.is_equal)
-        tt(C(12), C(10), C(11), O.add)
-        tt(C(13), C(12), C(9), O.add)
-        ts(A("col", 18, 21), A("col", 12, 15), PH, O.mult)
-        tt(A("col", 15, 18), A("col", 12, 15), A("col", 18, 21), O.subtract)
-        for k in range(3):
-            for h in range(2):
-                w = 15 + 3 * h + k
-                ts(A("selx", 128 * (2 * k + h), 128 * (2 * k + h) + 128, 1, 0, 64), A("l4", 0, 128, 1, 0, 64),
-                   A("col", 3, 4, 1, 0, 64), O.is_equal, A("col", w, w + 1, 1, 0, 64), O.mult)
+        ts(C(10), PD, 0.0, O.is_equal, 4096.0, O.mult)
+        ts(C(11), PD, 1.0, O.is_equal, 64.0, O.mult)
+        ts(C(12), PD, 2.0, O.is_equal)
+        ts(C(13), PD, 3.0, O.is_equal, 8192.0, O.mult)
+        ts(A("selb", 0, 128, 1, 0, 32), A("l4", 0, 128, 1, 0, 32), C(3, 32), O.is_equal)
+        ts(NNEG, NONEC, -1.0, O.mult)
+        ts(N9, NONEC, 9.0, O.mult)
+        tt(C(14), C(11), C(12), O.add)
         ts(A("dumpB", 0, 16), A("l16", 0, 16), PM, O.add, 1025.0, O.add)
         ts(A("dumpA", 0, 16), A("l16", 0, 16), PM, O.add, 3200.0, O.add)
-        prefill(0)
+        tt(C(15), C(14), C(13), O.add)
+        tt(C(16), C(14), C(10), O.add)
 
-    def prefill(k):
-        for r in range(8):
-            fill(A("win%d" % k, 256 * r + 1, 256 * r + 33), float(1024 * r + 1025))
+    def late_scalar():
+        act(A("bs64", 0, 8), blksel, F.Copy, scale=65536.0)
+        act(A("blk8", 0, 128), A("blk1", 0, 128), F.Copy, scale=8.0)
+        act(A("woff", 0, 128), A("blk1", 0, 128), F.Copy, scale=J256)
+        act(A("selL", 0, 128, 1, 0, 32), A("selb", 0, 128, 1, 0, 32), F.Copy, scale=C(15, 32))
+        act(A("selC", 0, 128, 1, 0, 32), A("selb", 0, 128, 1, 0, 32), F.Copy, scale=C(16, 32))
 
-    def pair_ops(sc, sbase, u16, x, half_pairs):
-        tt(A("eqd", 0, 256), A(sc, sbase, sbase + 256), x, O.is_equal)
+    def pairs(sc, base, u16):
         for a in range(15):
-            c = sbase + 16 * a + 15
+            c = base + 16 * a + 15
             ts(A("eqx", 256 * a + 16 * (a + 1), 256 * a + 256), A(u16, 16 * (a + 1), 256), A(sc, c, c + 1), O.is_equal)
 
     for st in range(3):
         last = st == 2
+        win, land = "win%d" % st, "land%d" % st
+        base = 1 if st == 0 else 1 + 1024 * me
+        x = "xz" if st == 0 else "xi"
         if st == 0:
             ts(A("wkf", 0, 256, 1, 0, 8), A("wkb", 0, 256, 1, 0, 8), 1.0, O.add)
             mm(A("b4", 256, 512), A("sel8", 0, 128, 1, 0, 8), A("wkf", 0, 256, 1, 0, 8), True, True)
-            cp(A("xz", 0, 256), A("b4", 256, 512))
-            x, base = A("xz", 0, 256), 1
+            for h in range(2):
+                cp(H("xz", h), H("b4", h, 256))
         else:
-            cp(A("ci", 0, 256), A("land%d" % (st - 1), 0, 256))
-            ts(A("xi", 0, 256), A("ci", 0, 256), 16383, O.bitwise_and)
-            x, base = A("xi", 0, 256), 1 + 1024 * me
-        tt(A("M1", 0, 256), x, maskP, O.mult)
-        scan(SC, A("rst", 0, 256), A("M1", 0, 256))
+            old = "land%d" % (st - 1)
+            act(A("cm", 0, 256), A(old, 0, 256), F.Identity, bias=MAGIC, scale=1.0 / 16384)
+            act(A("cB", 0, 256), A("cm", 0, 256), F.Identity, bias=-MAGIC)
+            for h in range(2):
+                ts(H("ci", h), H(old, h), 4096.0, O.add)
+            for h in range(2):
+                ts(H("xi", h), H("ci", h), 16383, O.bitwise_and)
+        for h in range(2):
+            tt(H("M1", h), H(x, h), maskP(h), O.mult)
+        for h in range(2):
+            scan(SC(h), H("rst", h), H("M1", h))
         scW = A("b2", 256 + 15, 512, 16)
         ts(A("BWu", 0, 16), scW, float(-base), O.add)
         BW = A("BWu", 0, 16)
 
-        def dedup1():
-            cp(A("xu", 0, 256), x)
-            pair_ops("b2", 256, "xu", x, True)
-
-        def dedup1_count():
-            for h in range(2):
-                out = A("b4", 16 + 8 * h, 24 + 8 * h)
-                mm(out, A("eqd", 128 * h, 128 * h + 128), A("bs1", 0, 8), True, False)
-                last_a = 7 if h == 0 else 15
-                for a in range(last_a):
-                    mm(out, A("eqx", 256 * a + 128 * h, 256 * a + 128 * h + 128), A("bs1", 0, 8), False, a == last_a - 1)
-
+        def eqd1(h):
+            tt(H("eqd", h), SC(h), H(x, h), O.is_equal)
         if st == 0:
-            dedup1()
+            for h in range(2):
+                cp(H("xu", h), H(x, h))
+            for h in range(2):
+                eqd1(h)
+            pairs("b2", 256, "xu")
             late_constants()
             cp(A("V2", 0, 256), IND(A("vt", 0, 1040), BW))
+            cp(A("Uo", 0, 256), IND(A("quS", 0, 1032), BW))
             ts(A("ut", 0, 1024), A("quS", 0, 1024), ADD1, O.add)
         else:
-            ts(A("cI", 0, 256), A("ci", 0, 256), 14, O.arith_shift_right)
-            tt(A("V1", 0, 256), IND(A("vt", 0, 1040), BW), A("cI", 0, 256), O.subtract)
+            act(A("UI", 0, 256), IND(A("ut", 0, 1032), BW), F.Copy)
+            tt(A("V1", 0, 256), IND(A("vt", 0, 1040), BW), A("cB", 0, 256), O.subtract)
+            cp(H("xu", 0), H(x, 0))
             ts(A("V2", 0, 256), A("V1", 0, 256), -255.0, O.max)
-        act(A("UI", 0, 256), IND(A("ut", 0, 1032), BW), F.Copy)
-        for i in range(16):
+            ts(A("Uo", 0, 256), A("UI", 0, 256), NEG, O.add)
+            cp(H("xu", 1), H(x, 1))
+            for h in range(2):
+                eqd1(h)
+            pairs("b2", 256, "xu")
+        for i in range(16 - NV):
             act(A("NVx", i, 2048, 16), A("V2", 0, 128), F.Copy, scale=-1.0)
-        ts(A("Uo", 0, 256), IND(A("ut", 0, 1032), BW), NEG, O.add)
-        ts(A("neg", 0, 256), A("V2", 0, 256), 0.0, O.is_lt)
-        if st != 0:
-            dedup1()
-        NVP = A("b3", 0, 256)
-        act(NVP, A("V2", 0, 256), F.Copy, scale=-1.0)
-        for c in range(2):
-            act(A("Ag", 1024 * c, 1024 * c + 1024), IND(A("at", 0, 3200), A("Uo", 128 + 64 * c, 192 + 64 * c)), F.Copy)
+        for i in range(16 - NV, 16):
+            ts(A("NVx", i, 2048, 16), A("V2", 0, 128), -1.0, O.mult)
         act(A("NVr", 0, 256), A("V2", 0, 256), F.Relu, scale=-1.0)
+        if st == 0:
+            late_scalar()
+            act(A("UI", 0, 256), IND(A("ut", 0, 1032), BW), F.Copy)
+        act(A("b3", 128, XL), A("V2", 128, XL), F.Copy, scale=-1.0)
+        for c0, c1 in ((XL, 256), (128, 176), (176, XL)):
+            act(A("Ag", 16 * (c0 - 128), 16 * (c1 - 128)), IND(A("at", 0, 3200), A("Uo", c0, c1)), F.Copy)
         for h in range(2):
-            mm(A("b%d" % h, 0, 128), A("UI", 128 * h, 128 * h + 128), A("idF", 0, 128), True, False)
+            mm(A("b%d" % h, 0, 128), H("UI", h), A("idF", 0, 128), True, False)
         for h in range(2):
-            mm(A("b4", 8 * h, 8 * h + 8), A("neg", 128 * h, 128 * h + 128), A("bs1", 0, 8), True, True)
-        dedup1_count()
+            mm(A("b4", 8 * h, 8 * h + 8), H("NVr", h), blksel, True, True)
+        for h in range(2):
+            out = A("b4", 16 + 8 * h, 24 + 8 * h)
+            mm(out, H("eqd", h), blksel, True, False)
+            n = 7 if h == 0 else 15
+            for a in range(n):
+                mm(out, H("eqx", h, 256 * a), blksel, False, a == n - 1)
+        D0 = 16 * (XL - 128)
+        mm(A("b7", 0, 512), A("idB", 0, 128), A("Ag", D0, 2048), True, False)
+        for i in range(16):
+            mm(A("b7", i, 512, 16), A("idB", 0, 128), A("V2", XL, 256), False, i == 15)
+        act(A("ge1", D0, 2048), A("b7", 0, 512), F.Sign, bias=0.5)
         tt(A("ge0", 0, 2048), IND(A("at", 0, 3200), A("Uo", 0, 128)), A("NVx", 0, 2048), O.is_ge)
         for i in range(16):
             mm(A("b0", i, 128, 16), A("ge0", i, 2048, 16), A("bs64", 0, 8), False, i == 15)
-        act(A("so", 0, 64), A("b0", 1, 128, 2), F.Copy)
-        ts(A("sm", 0, 16), A("b4", 0, 16), 0.0, O.is_equal, float(XKEY), O.mult)
-        ts(A("sm", 16, 32), A("b4", 16, 32), 1.5, O.is_gt, float(XKEY), O.mult)
-        ts(A("digB", 48, 64), A("b4", 16, 32), 1.5, O.is_gt)
-        for i in range(16):
-            tt(A("ge1", 128 * i, 128 * i + 128), A("Ag", i, 2048, 16), A("b3", 128, 256), O.is_ge)
-            mm(A("b1", i, 128, 16), A("ge1", 128 * i, 128 * i + 128), A("bs64", 0, 8), False, i == 15)
-        act(A("so", 64, 128), A("b1", 1, 128, 2), F.Copy)
-        tt(A("sm", 32, 48), A("sm", 0, 16), A("sm", 16, 32), O.max)
-        tt(A("m1", 0, 64), A("b0", 0, 128, 2), A("so", 0, 64), O.max)
-        tt(A("m1", 64, 128), A("b1", 0, 128, 2), A("so", 64, 128), O.max)
-        tt(A("m2", 0, 64), A("m1", 0, 128, 2), A("m1", 1, 128, 2), O.max)
-        tt(A("m3", 0, 32), A("m2", 0, 64, 2), A("m2", 1, 64, 2), O.max)
-        tt(A("m4", 0, 16), A("m3", 0, 32, 2), A("m3", 1, 32, 2), O.max)
-        tt(A("ki", 0, 16), A("m4", 0, 16), A("sm", 32, 48), O.max)
-        ki = A("ki", 0, 16)
-        ts(A("digI", 16, 32), ki, 6, O.arith_shift_right, 63, O.bitwise_and)
-        ts(A("digI", 32, 48), ki, 63, O.bitwise_and)
-        ts(A("digI", 0, 16), ki, 12, O.arith_shift_right, 15, O.bitwise_and)
-        cp(A("digB", 0, 48), A("digI", 0, 48))
-        mm(A("b4", 128, 256, 1, 0, 64), A("digB", 0, 64), A("idB", 0, 128), True, True)
-        act(A("TTs", 0, 128, 1, 0, 64), A("b4", 128, 256, 1, 0, 64), F.Copy)
-        for k, (bank, c0) in enumerate((("b5", 0), ("b6", 0), ("b6", 256))):
-            for h in range(2):
-                mm(A(bank, c0 + 128 * h, c0 + 128 * h + 128), A("selx", 128 * (2 * k + h), 128 * (2 * k + h) + 128, 1, 0, 64),
-                   A("TTs", 0, 128, 1, 0, 64), True, True)
-        RL = A("b5", 0, 256)
-        tt(A("M5", 0, 256), RL, A("maskS", 0, 256), O.mult)
-        cp(A("Lu", 0, 256), RL)
-        scan(A("SC5", 0, 256), A("rst", 0, 256), A("M5", 0, 256))
-        l5 = A("SC5", 15, 256, 16)
-        pair_ops("SC5", 0, "Lu", RL, False)
-        ts(A("LWu", 0, 16), l5, -1.0, O.add)
-        LW = A("LWu", 0, 16)
-        CN = A("b7", 0, 256)
-        mm(CN, A("blk8", 0, 128), A("eqd", 0, 256), True, False)
+        ts(A("sm", 0, 16), A("b4", 0, 16), 0.0, O.is_equal, float(XKEY + LOW), O.mult)
+        ts(A("sm", 16, 32), A("b4", 16, 32), 1.5, O.is_gt, float(XKEY + LOW), O.mult)
+        for h in range(2):
+            ts(A("digB%d" % h, 24, 32), A("b4", 16 + 8 * h, 24 + 8 * h), 1.5, O.is_gt)
+        tt(A("sm", 160, 176), A("sm", 0, 16), A("sm", 16, 32), O.max)
+        ts(A("sm", 32, 48), A("sm", 160, 176), float(-LOW), O.add)
+        RL = (H("b5", 0), A("b0", 128, 256))
+
+        def best(h):
+            b, so, m = "b%d" % h, "so%d" % h, "mx%d" % h
+            ki, dI, dB, tp = A("ki%d" % h, 0, 8), "digI%d" % h, "digB%d" % h, A("b4", 128 + 128 * h, 256 + 128 * h, 1, 0, 32)
+            tr = A("TTs%d" % h, 0, 128, 1, 0, 32)
+
+            def m1():
+                act(A(so, 0, 64), A(b, 1, 128, 2), F.Copy)
+                tt(A(m, 0, 64), A(b, 0, 128, 2), A(so, 0, 64), O.max)
+
+            def to_r():
+                cp(A(dB, 0, 24), A(dI, 0, 24))
+                mm(tp, A(dB, 0, 32), A("idB", 0, 128), True, True)
+                act(tr, tp, F.Copy)
+                mm(RL[h], A("selL", 0, 128, 1, 0, 32), tr, True, True)
+                mm(H("b6", h, 256), A("selC", 0, 128, 1, 0, 32), tr, True, True)
+            return [m1,
+                    lambda: tt(A(m, 64, 96), A(m, 0, 64, 2), A(m, 1, 64, 2), O.max),
+                    lambda: tt(A(m, 96, 112), A(m, 64, 96, 2), A(m, 65, 96, 2), O.max),
+                    lambda: tt(A(m, 112, 120), A(m, 96, 112, 2), A(m, 97, 112, 2), O.max),
+                    lambda: tt(ki, A(m, 112, 120), A("sm", 32 + 8 * h, 40 + 8 * h), O.max),
+                    lambda: ts(A(dI, 8, 16), ki, 6, O.arith_shift_right, 63, O.bitwise_and),
+                    lambda: ts(A(dI, 16, 24), ki, 63, O.bitwise_and),
+                    lambda: ts(A(dI, 0, 8), ki, 12, O.arith_shift_right, 15, O.bitwise_and),
+                    to_r]
+
+        def lines(h):
+            lw = A("LWu", 8 * h, 8 * h + 8)
+
+            def draw():
+                tt(H("tt", h), IND(A("at", 0, 3200), lw), H("NVr", h), O.min)
+                act(H("t16", h), H("tt", h), F.Identity, bias=1.0 - 4096.0, scale=16384.0)
+            return [lambda: tt(H("M5", h), RL[h], H("maskS", h), O.mult),
+                    lambda: cp(H("Lu", h), RL[h]),
+                    lambda: scan(H("SC5", h), H("rst", h), H("M5", h)),
+                    lambda: tt(H("eqe", h), H("SC5", h), RL[h], O.is_equal),
+                    lambda: ts(lw, A("SC5", 128 * h + 15, 128 * h + 128, 16), float(NONE1), O.min, -1.0, O.add),
+                    draw,
+                    lambda: cp(H("payf", h), IND(A("pt", 0, 3200), lw)),
+                    lambda: ts(H("r8", h), H("payf", h), 1.0 / 1024, O.mult, -511.5 / 1024 - 8.0, O.add)]
+
+        def ge1(i):
+            tt(A("ge1", i, D0, 16), A("Ag", i, D0, 16), A("b3", 128, XL), O.is_ge)
+            mm(A("b1", i, 128, 16), A("ge1", i, 2048, 16), A("bs64", 0, 8), False, i == 15)
+        best0, best1, lines0, lines1 = best(0), best(1), lines(0), lines(1)
+        weave([lambda i=i: ge1(i) for i in range(16)], best0[:6], 12)
+        weave(best1, best0[6:], 0)
+        for f in lines0[:6 if st == 0 else 8] + lines1[:5]:
+            f()
+        pairs("SC5", 0, "Lu")
+        CN = (A("b6", 0, 128), A("b7", 0, 128))
+        mm(CN[0], A("blk8", 0, 128), H("eqe", 0), True, False)
+        mm(CN[1], A("blk8", 0, 128), H("eqe", 1), True, False)
         for a in range(15):
-            mm(A("b7", 16 * (a + 1), 256), A("blk8", 0, 128), A("eqx", 256 * a + 16 * (a + 1), 256 * a + 256), False, a == 14)
+            if a < 7:
+                mm(A("b6", 16 * (a + 1), 128), A("blk8", 0, 128), A("eqx", 256 * a + 16 * (a + 1), 256 * a + 128), False, a == 6)
+            lo = max(128, 16 * (a + 1))
+            mm(A("b7", lo - 128, 128), A("blk8", 0, 128), A("eqx", 256 * a + lo, 256 * a + 256), False, a == 14)
         if st == 0:
             fill(A("pt", 3199, 3200), 8192)
-        cp(A("payf", 0, 256), IND(A("pt", 0, 3200), LW))
-        tt(A("tt", 0, 256), IND(A("at", 0, 3200), LW), A("NVr", 0, 256), O.min)
-        ts(A("r8", 0, 256), A("payf", 0, 256), 1.0 / 1024, O.mult, -511.5 / 1024 - 8.0, O.add)
-        act(A("t16", 0, 256), A("tt", 0, 256), F.Identity, bias=1.0, scale=16384.0)
-        if not last:
-            act(A("Agl", 0, 256), IND(A("at", 0, 3200), LW), F.Copy)
-        tt(A("zz", 0, 256), CN, A("r8", 0, 256), O.add)
-        OH, cum = A("OH", 0, 256), A("b3", 256, 512)
-        ts(OH, A("zz", 0, 256), 8.0, O.min, PM, O.is_equal)
-        scan(cum, A("ones", 0, 256), OH)
-        OFF = A("b5", 256, 512)
-        mm(OFF, A("woff", 0, 128), OH, True, False)
-        tt(A("prod", 0, 256), cum, OH, O.mult)
-        mm(OFF, A("blk1", 0, 128), A("prod", 0, 256), False, True)
-        tt(A("M6", 0, 256), OFF, A("maskS", 0, 256), O.mult)
-        scan(A("SC6", 0, 256), A("rst", 0, 256), A("M6", 0, 256))
-        o6 = A("SC6", 15, 256, 16)
+            lines0[6]()
+            lines0[7]()
+        for f in lines1[5:]:
+            f()
+        cum = lambda h: H("b3", h, 256)
+        OFF = (A("b5", 256, 384), A("b1", 256, 384))
+        for h in range(2):
+            tt(H("zz", h), CN[h], H("r8", h), O.add)
+        for h in range(2):
+            ts(H("OH", h), H("zz", h), 8.0, O.min, PM, O.is_equal)
+            mm(OFF[h], A("woff", 0, 128), H("OH", h), True, False)
+        scan(cum(0), H("ones", 0), H("OH", 0))
+        tt(H("prod", 0), cum(0), H("OH", 0), O.mult)
+        scan(cum(1), H("ones", 1), H("OH", 1), A("b3", 383, 384))
+        mm(OFF[0], A("blk1", 0, 128), H("prod", 0), False, True)
+        tt(H("prod", 1), cum(1), H("OH", 1), O.mult)
+        mm(OFF[1], A("blk1", 0, 128), H("prod", 1), False, True)
+        for h in range(2):
+            act(H("b3", h, 256), CN[h], F.Relu, bias=9.0, scale=-1.0)
+        tm = A("b3", 0, 256)
+        tt(H("M6", 0), OFF[0], H("maskS", 0), O.mult)
+        tt(H("M6", 1), OFF[1], H("maskS", 1), O.mult)
+        for h in range(2):
+            scan(H("SC6", h), H("rst", h), H("M6", h))
+        o6, l5 = A("SC6", 15, 256, 16), A("SC5", 15, 256, 16)
+        ts(A("sm", 64, 80), scW, float(-base), O.add)
+        ts(A("sm", 48, 64), l5, 4096.0, O.is_gt)
         cp(A("OWu", 0, 16), o6)
-        win, land = "win%d" % st, "land%d" % st
         tt(IND(A(win, 0, WIN), A("OWu", 0, 16)), A("t16", 0, 256), A("payf", 0, 256), O.add)
         sync_for(P, "g", [(win, 0, WIN, 1)], [])
-        mk = masks(topo, T.cores, me)
-        transfers = []
-        for k in range(1, 8):
-            r = (me + k) % 8
-            rid, pid = topo.addr(T.cores[r], core)
-            transfers.append(RemoteDMATransfer(dst_ids=[DstId(rid=rid, pnc=pid)], dma_engine_mask=sum(1 << e for e in mk[r]),
-                                               remote_sem=T.sem["arr%d" % st], src=T[win][:, 256 * r + 1:256 * r + 33],
-                                               dst=T[land][:, 32 * me:32 * me + 32]))
-        g.remote_dma_fused(transfers, local_sem=T.sem["loc"])
-        note(P, "g", [(win, 0, WIN, 1)], [], "loc", (st + 1) * sum(len(mk[r]) for r in mk))
-        arrive = sum(len(masks(topo, T.cores, q)[me]) for q in range(8) if q != me)
+        calls = plan(topo, T.cores, me)
+        for c in calls:
+            g.remote_dma_fused([RemoteDMATransfer(
+                dst_ids=[DstId(rid=topo.addr(T.cores[r], core)[0], pnc=topo.addr(T.cores[r], core)[1])],
+                dma_engine_mask=sum(1 << e for e in engines), remote_sem=T.sem["arr%d" % st],
+                src=T[win][:, 256 * r + 1:256 * r + 33], dst=T[land][:, 32 * me:32 * me + 32])
+                for r, engines in c], local_sem=T.sem["loc"])
+        out_n = sum(len(e) for c in calls for r, e in c)
+        arrive = sum(len(e) for q in range(8) if q != me for c in plan(topo, T.cores, q) for r, e in c if r == me)
         for q in range(8):
             if q != me:
                 note(P, "remote", [], [(land, 32 * q, 32 * q + 32, 1)], "arr%d" % st, arrive)
         cp(A(land, 32 * me, 32 * me + 32), A(win, 256 * me + 1, 256 * me + 33))
-        okP = A("b3", 256, 512)
-        ts(okP, CN, 8.0, O.is_equal)
-        RD = A("b6", 256, 512)
-        tt(A("M7", 0, 256), RD, A("maskS", 0, 256), O.mult)
-        tt(A("tm", 0, 256), okP, A("tt", 0, 256), O.mult)
-        scan(A("SC7", 0, 256), A("rst", 0, 256), A("M7", 0, 256))
-        tt(A("Vn", 0, 256), A("tm", 0, 256), NVP, O.subtract)
-        tt(A("sm", 48, 64), A("SC7", 15, 256, 16), A("dumpB", 0, 16), O.mult)
-        ts(A("sm", 64, 80), scW, float(-base), O.add)
+        tt(tm, A("b3", 256, 512), A("tt", 0, 256), O.mult)
+        tt(A("sm", 48, 64), A("sm", 48, 64), A("dumpB", 0, 16), O.mult)
+        tt(A("Vn", 0, 256), tm, A("V2", 0, 256), O.add)
         tt(A("sm", 80, 96), A("sm", 48, 64), A("sm", 64, 80), O.max)
+        if not last:
+            tt(A("OHu", 0, 256), A("b6", 256, 512), A("UI", 0, 256), O.is_equal)
         cp(A("boU", 0, 16), A("sm", 80, 96))
+        if not last:
+            act(A("Agl", 0, 256), IND(A("at", 0, 3200), A("LWu", 0, 16)), F.Copy)
+            for h in range(2):
+                act(H("b7", h, 128), CN[h], F.Relu, bias=N9, scale=NNEG)
+            ts(A("sm", 96, 112), o6, 2048.5, O.is_gt)
+            ts(A("sm", 112, 128), l5, float(NONE1), O.min, -1.0, O.add)
         cp(IND(A("vt", 0, 1296), A("boU", 0, 16)), A("Vn", 0, 256))
         if last:
             break
-        okX = A("b7", 256, 512)
-        ts(okX, CN, 8.0, O.is_equal, NONEC, O.mult)
-        tt(A("OHu", 0, 256), A("b6", 0, 256), A("UI", 0, 256), O.is_equal)
-        ts(A("sm", 96, 112), o6, 2048.5, O.is_gt)
-        tt(A("OHk", 0, 256), okX, A("OHu", 0, 256), O.mult)
-        ts(A("sm", 112, 128), l5, -1.0, O.add)
-        tt(A("UIn", 0, 256), A("UI", 0, 256), A("OHk", 0, 256), O.max)
-        tt(A("sm", 96, 112), A("sm", 96, 112), A("dumpA", 0, 16), O.mult)
-        tt(A("An", 0, 256), A("Agl", 0, 256), A("tm", 0, 256), O.subtract)
-        tt(A("sm", 96, 112), A("sm", 96, 112), A("sm", 112, 128), O.max)
+        okX = A("b7", 128, 384)
+        tt(okX, okX, A("OHu", 0, 256), O.mult)
+        tt(A("sm", 128, 144), A("sm", 96, 112), A("dumpA", 0, 16), O.mult)
+        tt(A("UIn", 0, 256), A("UI", 0, 256), okX, O.max)
+        tt(A("sm", 144, 160), A("sm", 128, 144), A("sm", 112, 128), O.max)
+        tt(A("An", 0, 256), A("Agl", 0, 256), tm, O.subtract)
+        cp(A("aoU", 0, 16), A("sm", 144, 160))
         cp(IND(A("ut", 0, 1296), A("boU", 0, 16)), A("UIn", 0, 256))
-        cp(A("aoU", 0, 16), A("sm", 96, 112))
         cp(IND(A("at", 0, 3456), A("aoU", 0, 16)), A("An", 0, 256))
-        prefill(st + 1)
 
-    def store(q, dst, src_view, sem):
-        sync_for(P, q, regions([src_view]), [])
-        P["eng"][q].dma_start(dst, resolve(P, src_view)).then_inc(T.sem[sem], 16)
-    store("y", T.yv[:], A("vt", 0, 1024), "dyv")
-    cp(A("ci", 0, 256), A("land2", 0, 256))
-    ts(A("xi", 0, 256), A("ci", 0, 256), 16383, O.bitwise_and)
-    ts(A("cI", 0, 256), A("ci", 0, 256), 14, O.arith_shift_right)
-    ts(A("ywS", 0, 256), A("xi", 0, 256), float(-(1 + 1024 * me)), O.add)
-    store("y", T.yw[:], A("ywS", 0, 256, 1, 0, 128)[:5] + ((0, 128)) if False else A("ywS", 0, 256), "dyw") if False else None
+    sync_for(P, "y", [("vt", 0, 1024, 1)], [])
+    y.dma_start(T.yv[:], T.vt[:, 0:1024]).then_inc(T.sem["dyv"], 16)
+    act(A("cm", 0, 256), A("land2", 0, 256), F.Identity, bias=MAGIC, scale=1.0 / 16384)
+    act(A("cB", 0, 256), A("cm", 0, 256), F.Identity, bias=-MAGIC)
+    for h in range(2):
+        ts(H("ci", h), H("land2", h), 4096.0, O.add)
+    for h in range(2):
+        ts(H("xi", h), H("ci", h), 16383, O.bitwise_and)
+    for h in range(2):
+        ts(H("ywS", h), H("xi", h), float(-(1 + 1024 * me)), O.add)
+    sync_for(P, "s", regions([A("cB", 0, 256)]), [])
+    s.dma_start(T.yc[:], T.cB[:, 0:256]).then_inc(T.sem["dyc"], 16)
     sync_for(P, "y", regions([A("ywS", 0, 256)]), [])
     y.dma_start(T.yw[:], T.ywS[0:128:16, 0:256]).then_inc(T.sem["dyw"], 16)
-    cp(A("ycS", 0, 256), A("cI", 0, 256))
-    store("s", T.yc[:], A("ycS", 0, 256), "dyc")
     for sem in ("sv", "ss", "sp", "sg"):
         g.wait_ge(T.sem[sem], P["cnt"][sem])
     for sem in ("dwk", "dvp", "dqu", "dam", "dyv", "dyw", "dyc"):
         g.wait_ge(T.sem[sem], 16)
     g.wait_ge(T.sem["dpay"], 256)
-    g.wait_ge(T.sem["loc"], 3 * sum(len(mk[r]) for r in mk))
+    g.wait_ge(T.sem["loc"], 3 * out_n)
     for k in range(3):
         g.wait_ge(T.sem["arr%d" % k], arrive)
 
 
-def masks(topo, cores, q):
+def plan(topo, cores, q):
     src = cores[q]
-    others = [r for r in range(len(cores)) if r != q]
+    others = [(q + k) % len(cores) for k in range(1, len(cores))]
     near = [r for r in others if cores[r] in topo.cores_of(src)]
     far = [r for r in others if r not in near]
-    free = list(topo.engines(src, cores[far[0]]))
-    out = {}
-    for r in far:
-        e = [x for x in free if x in topo.engines(src, cores[r])][0]
-        out[r] = [e]
-        free.remove(e)
-    for n, r in enumerate(near):
-        k = len(free) // (len(near) - n)
-        while k & (k - 1):
-            k -= 1
-        out[r] = free[:k]
-        free = free[k:]
-    return out
+    far.sort(key=lambda r: topo.same_plane(src, cores[r]) or topo.mates(src, cores[r]))
+    out = [e for e in topo.engines(src, cores[far[0]])]
+    inside = [e for e in topo.engines(src, cores[near[0]]) if e not in out]
+    n = len(out) // 4
+    first = [(r, out[n * k:n * k + n]) for k, r in enumerate(far[:4])]
+    first += [(r, inside[n * k:n * k + n]) for k, r in enumerate(near)]
+    m = len(out) // 2
+    return [first, [(r, out[m * k:m * k + m]) for k, r in enumerate(far[4:])]]

@@ -3,11 +3,11 @@ from concourse.mybir import AluOpType as O, ActivationFunctionType as F
 
 WIN = 2312
 SCRATCH = {}
-for _n in "wkb ci xi r8".split():
+for _n in "wkb ci xi".split():
     SCRATCH[_n] = ("sbuf", [128, 256], "int32")
-for _n in "wkf xz UI M1 M5 M6 SC5 SC6 t16 payf OHu UIn ywS cm land0 land1 land2".split():
+for _n in "wkf xz UI M1 M5 M6 SC5 SC6 t16 payf payg OHu UIn ywS cm land0 land1 land2".split():
     SCRATCH[_n] = ("sbuf", [128, 256], "float32")
-for _n in "maskS rst ones V1 V2 NVr eqd eqe tt zz OH prod Vn An Agl cB".split():
+for _n in "maskS rst ones V1 V2 NVr eqd eqe tt r8 sgn OH prod Vn An Agl cB".split():
     SCRATCH[_n] = ("sbuf", [128, 256], "bfloat16")
 for _n in "blk1 blkT blk8 woff idB selb selL selC TTs0 TTs1".split():
     SCRATCH[_n] = ("sbuf", [128, 128], "bfloat16")
@@ -17,7 +17,7 @@ for _n in "xu Lu Uo".split():
     SCRATCH[_n] = ("sbuf", [128, 256], "uint16")
 for _n in "NVx ge0 Ag ge1".split():
     SCRATCH[_n] = ("sbuf", [128, 2048], "bfloat16")
-for _n in "onesF idF sel8 selT".split():
+for _n in "onesF idF sel8 selT row0".split():
     SCRATCH[_n] = ("sbuf", [128, 128], "float32")
 for _n in range(3):
     SCRATCH["win%d" % _n] = ("sbuf", [128, WIN], "float32")
@@ -34,6 +34,7 @@ SCRATCH["ut"] = ("sbuf", [128, 1296], "float32")
 SCRATCH["vt"] = ("sbuf", [128, 1296], "bfloat16")
 SCRATCH["at"] = ("sbuf", [128, 3456], "bfloat16")
 SCRATCH["pt"] = ("sbuf", [128, 3200], "int32")
+SCRATCH["pq"] = ("sbuf", [128, 3200], "int32")
 SCRATCH["eqx"] = ("sbuf", [128, 3840], "bfloat16")
 SCRATCH["l15"] = ("sbuf", [128, 256], "int32")
 SCRATCH["l4"] = ("sbuf", [128, 128], "int32")
@@ -44,13 +45,17 @@ SCRATCH["bs64"] = ("sbuf", [128, 8], "bfloat16")
 SCRATCH["dumpA"] = ("sbuf", [128, 16], "float32")
 SCRATCH["dumpB"] = ("sbuf", [128, 16], "float32")
 SCRATCH["sm"] = ("sbuf", [128, 192], "float32")
-SEMAPHORES = ["sv", "ss", "sp", "sg", "dwk", "dvp", "dqu", "dam", "dpay", "dyv", "dyw", "dyc", "loc", "arr0", "arr1", "arr2"]
+SEMAPHORES = ["sv", "ss", "sp", "sg", "dwk", "dvp", "dqu", "dam", "dpq", "dpay", "dyv", "dyw", "dyc", "loc", "arr0", "arr1", "arr2"]
 NONE1 = 3200
 XKEY = 272 * 4096 + NONE1
 LOW = 2097152
+HALF = (XKEY + LOW) / 2.0
 MAGIC = 12582912.0
 XL = 224
-NV = 4
+NV = 5
+ODD = list(range(1, 16, 2)) + list(range(0, 16, 2))
+ORDER0 = "a0 a1 a2 a4 a6 a7 a3 P0 a8 b0 b1 b2 b4 b6 b7 b3 P1 b8 a9 aa a5 ab b5 b9 ba bb".split()
+ORDER = "a0 a1 a2 a3 a4 P0 a6 a7 a8 b0 b1 b2 b3 b4 P1 b6 b7 b8 a9 aa a5 ab b5 b9 ba bb".split()
 
 
 def A(name, c0, c1, step=1, p0=0, p1=128):
@@ -59,6 +64,14 @@ def A(name, c0, c1, step=1, p0=0, p1=128):
 
 def IND(win, off):
     return ("I", win, off)
+
+
+KB = ((A("b0", 0, 64), A("b5", 384, 448)), (A("b1", 0, 64), A("b6", 128, 192)))
+
+
+def KI(h, i):
+    k = KB[h][i % 2]
+    return A(k[1], k[2] + i // 2, k[3], 8)
 
 
 def is_view(x):
@@ -191,9 +204,6 @@ def rank_program(g, core, T, topo):
     load("s", A("vt", 0, 1024), T.vp[:], "dvp")
     load("y", A("quS", 0, 1024), T.qu[:], "dqu")
     load("y", A("at", 0, 3200), T.am[:], "dam")
-    for j in range(16):
-        y.dma_start(T.pt[j:128:16, :], T.pay[:]).then_inc(T.sem["dpay"], 16)
-    note(P, "dpay", [], [("pt", 0, 3200, 1)], "dpay", 256)
 
     imp = {"allow_small_or_imprecise_dtypes": True}
     iota(A("pci", 0, 1), [[1, 1]], 0, 1)
@@ -201,13 +211,21 @@ def rank_program(g, core, T, topo):
     iota(A("onesF", 0, 128), [[0, 128]], 1, 0, **imp)
     pick(A("selT", 0, 128, 1, 0, 8), A("onesF", 0, 128, 1, 0, 8), [[1, 128]], O.is_ge, 0, -16)
     pick(A("sel8", 0, 128, 1, 0, 8), A("selT", 0, 128, 1, 0, 8), [[-1, 128]], O.is_ge, 15, 16)
+    iota(A("l4", 0, 128), [[1, 8], [0, 16]], 0, 0)
+    iota(A("l16", 0, 16), [[16, 16]], 0, 0)
     iota(A("ones", 0, 256), [[0, 256]], 1, 0, **imp)
     pick(A("blkT", 0, 128), A("ones", 0, 128), [[-16, 8], [0, 16]], O.is_ge, 0, 1)
     pick(A("blk1", 0, 128), A("blkT", 0, 128), [[16, 8], [0, 16]], O.is_ge, 15, -1)
     pick(A("idF", 0, 128), A("onesF", 0, 128), [[-1, 128]], O.is_equal, 0, 1)
+    pick(A("row0", 0, 128), A("onesF", 0, 128), [[-16, 8], [0, 16]], O.is_equal, 0, 1)
     pick(A("idB", 0, 128), A("ones", 0, 128), [[-1, 128]], O.is_equal, 0, 1)
-    iota(A("l4", 0, 128), [[1, 8], [0, 16]], 0, 0)
-    iota(A("l16", 0, 16), [[16, 16]], 0, 0)
+    iota(A("pq", 0, 3200), [[0, 3200]], 0, 0)
+    sync_for(P, "y", [], [("pq", 0, 3200, 1)])
+    y.dma_start(T.pq[0:128:16, :], T.pay[:]).then_inc(T.sem["dpq"], 16)
+    note(P, "dpq", [], [("pq", 0, 3200, 1)], "dpq", 16)
+    for j in range(16):
+        y.dma_start(T.pt[j:128:16, :], T.pay[:]).then_inc(T.sem["dpay"], 16)
+    note(P, "dpay", [], [("pt", 0, 3200, 1)], "dpay", 256)
     for k in range(3):
         for r in range(8):
             iota(A("win%d" % k, 256 * r + 1, 256 * r + 33), [[0, 32]], 1024 * r + 1025 - 4096, 0, **imp)
@@ -217,7 +235,7 @@ def rank_program(g, core, T, topo):
     ts(A("pci", 3, 4), p0, 7, O.bitwise_and)
     cp(A("col", 0, 4), A("pci", 0, 4))
     PM, PD = C(1), C(2)
-    ADD1, NONEC, NNEG, N9, J256, NEG = C(4), C(5), C(6), C(7), C(8), C(9)
+    ADD1, NONEC, J256, NEG = C(4), C(5), C(8), C(9)
     maskP = lambda h: H("b2", h)
     SC = lambda h: H("b2", h, 256)
     ts(A("b2", 0, 256), A("l15", 0, 256), PM, O.is_equal)
@@ -240,8 +258,6 @@ def rank_program(g, core, T, topo):
         ts(C(12), PD, 2.0, O.is_equal)
         ts(C(13), PD, 3.0, O.is_equal, 8192.0, O.mult)
         ts(A("selb", 0, 128, 1, 0, 32), A("l4", 0, 128, 1, 0, 32), C(3, 32), O.is_equal)
-        ts(NNEG, NONEC, -1.0, O.mult)
-        ts(N9, NONEC, 9.0, O.mult)
         tt(C(14), C(11), C(12), O.add)
         ts(A("dumpB", 0, 16), A("l16", 0, 16), PM, O.add, 1025.0, O.add)
         ts(A("dumpA", 0, 16), A("l16", 0, 16), PM, O.add, 3200.0, O.add)
@@ -255,10 +271,10 @@ def rank_program(g, core, T, topo):
         act(A("selL", 0, 128, 1, 0, 32), A("selb", 0, 128, 1, 0, 32), F.Copy, scale=C(15, 32))
         act(A("selC", 0, 128, 1, 0, 32), A("selb", 0, 128, 1, 0, 32), F.Copy, scale=C(16, 32))
 
-    def pairs(sc, base, u16):
+    def pairs1():
         for a in range(15):
-            c = base + 16 * a + 15
-            ts(A("eqx", 256 * a + 16 * (a + 1), 256 * a + 256), A(u16, 16 * (a + 1), 256), A(sc, c, c + 1), O.is_equal)
+            c = 256 + 16 * a + 15
+            ts(A("eqx", 256 * a + 16 * (a + 1), 256 * a + 256), A("xu", 16 * (a + 1), 256), A("b2", c, c + 1), O.is_equal)
 
     for st in range(3):
         last = st == 2
@@ -268,6 +284,7 @@ def rank_program(g, core, T, topo):
         if st == 0:
             ts(A("wkf", 0, 256, 1, 0, 8), A("wkb", 0, 256, 1, 0, 8), 1.0, O.add)
             mm(A("b4", 256, 512), A("sel8", 0, 128, 1, 0, 8), A("wkf", 0, 256, 1, 0, 8), True, True)
+            late_constants()
             for h in range(2):
                 cp(H("xz", h), H("b4", h, 256))
         else:
@@ -289,15 +306,15 @@ def rank_program(g, core, T, topo):
         def eqd1(h):
             tt(H("eqd", h), SC(h), H(x, h), O.is_equal)
         if st == 0:
+            cp(A("V2", 0, 256), IND(A("vt", 0, 1040), BW))
             for h in range(2):
                 cp(H("xu", h), H(x, h))
             for h in range(2):
                 eqd1(h)
-            pairs("b2", 256, "xu")
-            late_constants()
-            cp(A("V2", 0, 256), IND(A("vt", 0, 1040), BW))
+            pairs1()
             cp(A("Uo", 0, 256), IND(A("quS", 0, 1032), BW))
             ts(A("ut", 0, 1024), A("quS", 0, 1024), ADD1, O.add)
+            late_scalar()
         else:
             act(A("UI", 0, 256), IND(A("ut", 0, 1032), BW), F.Copy)
             tt(A("V1", 0, 256), IND(A("vt", 0, 1040), BW), A("cB", 0, 256), O.subtract)
@@ -307,20 +324,20 @@ def rank_program(g, core, T, topo):
             cp(H("xu", 1), H(x, 1))
             for h in range(2):
                 eqd1(h)
-            pairs("b2", 256, "xu")
+            pairs1()
         for i in range(16 - NV):
             act(A("NVx", i, 2048, 16), A("V2", 0, 128), F.Copy, scale=-1.0)
         for i in range(16 - NV, 16):
             ts(A("NVx", i, 2048, 16), A("V2", 0, 128), -1.0, O.mult)
         act(A("NVr", 0, 256), A("V2", 0, 256), F.Relu, scale=-1.0)
         if st == 0:
-            late_scalar()
             act(A("UI", 0, 256), IND(A("ut", 0, 1032), BW), F.Copy)
         act(A("b3", 128, XL), A("V2", 128, XL), F.Copy, scale=-1.0)
         for c0, c1 in ((XL, 256), (128, 176), (176, XL)):
             act(A("Ag", 16 * (c0 - 128), 16 * (c1 - 128)), IND(A("at", 0, 3200), A("Uo", c0, c1)), F.Copy)
         for h in range(2):
-            mm(A("b%d" % h, 0, 128), H("UI", h), A("idF", 0, 128), True, False)
+            for e in range(2):
+                mm(KB[h][e], H("UI", h), A("idF", e, 128, 2), True, False)
         for h in range(2):
             mm(A("b4", 8 * h, 8 * h + 8), H("NVr", h), blksel, True, True)
         for h in range(2):
@@ -335,94 +352,116 @@ def rank_program(g, core, T, topo):
             mm(A("b7", i, 512, 16), A("idB", 0, 128), A("V2", XL, 256), False, i == 15)
         act(A("ge1", D0, 2048), A("b7", 0, 512), F.Sign, bias=0.5)
         tt(A("ge0", 0, 2048), IND(A("at", 0, 3200), A("Uo", 0, 128)), A("NVx", 0, 2048), O.is_ge)
-        for i in range(16):
-            mm(A("b0", i, 128, 16), A("ge0", i, 2048, 16), A("bs64", 0, 8), False, i == 15)
-        ts(A("sm", 0, 16), A("b4", 0, 16), 0.0, O.is_equal, float(XKEY + LOW), O.mult)
-        ts(A("sm", 16, 32), A("b4", 16, 32), 1.5, O.is_gt, float(XKEY + LOW), O.mult)
+        for i in ODD:
+            mm(KI(0, i), A("ge0", i, 2048, 16), A("bs64", 0, 8), False, i >= 14)
+        act(A("so0", 0, 64), KB[0][1], F.Copy)
+        act(A("sm", 0, 16), A("b4", 0, 16), F.Sign, bias=-0.5)
+        act(A("sm", 16, 32), A("b4", 16, 32), F.Sign, bias=-1.5)
         for h in range(2):
-            ts(A("digB%d" % h, 24, 32), A("b4", 16 + 8 * h, 24 + 8 * h), 1.5, O.is_gt)
-        tt(A("sm", 160, 176), A("sm", 0, 16), A("sm", 16, 32), O.max)
-        ts(A("sm", 32, 48), A("sm", 160, 176), float(-LOW), O.add)
+            act(A("digB%d" % h, 24, 32), A("sm", 16 + 8 * h, 24 + 8 * h), F.Relu)
+        act(A("sm", 160, 176), A("sm", 0, 16), F.Identity, bias=HALF - LOW, scale=-HALF)
+        act(A("sm", 176, 192), A("sm", 16, 32), F.Identity, bias=HALF - LOW, scale=HALF)
         RL = (H("b5", 0), A("b0", 128, 256))
+        CN = (A("b6", 0, 128), A("b7", 0, 128))
+        OFF = (A("b5", 256, 384), A("b1", 256, 384))
 
         def best(h):
-            b, so, m = "b%d" % h, "so%d" % h, "mx%d" % h
+            m = "mx%d" % h
             ki, dI, dB, tp = A("ki%d" % h, 0, 8), "digI%d" % h, "digB%d" % h, A("b4", 128 + 128 * h, 256 + 128 * h, 1, 0, 32)
             tr = A("TTs%d" % h, 0, 128, 1, 0, 32)
 
-            def m1():
-                act(A(so, 0, 64), A(b, 1, 128, 2), F.Copy)
-                tt(A(m, 0, 64), A(b, 0, 128, 2), A(so, 0, 64), O.max)
+            def row_digit():
+                if not last:
+                    ts(A(dI, 0, 8), ki, 12, O.arith_shift_right, 15, O.bitwise_and)
 
             def to_r():
                 cp(A(dB, 0, 24), A(dI, 0, 24))
                 mm(tp, A(dB, 0, 32), A("idB", 0, 128), True, True)
                 act(tr, tp, F.Copy)
                 mm(RL[h], A("selL", 0, 128, 1, 0, 32), tr, True, True)
-                mm(H("b6", h, 256), A("selC", 0, 128, 1, 0, 32), tr, True, True)
-            return [m1,
+                if not last:
+                    mm(H("b6", h, 256), A("selC", 0, 128, 1, 0, 32), tr, True, True)
+            return [lambda: tt(A(m, 0, 64), KB[h][0], A("so%d" % h, 0, 64), O.max),
                     lambda: tt(A(m, 64, 96), A(m, 0, 64, 2), A(m, 1, 64, 2), O.max),
                     lambda: tt(A(m, 96, 112), A(m, 64, 96, 2), A(m, 65, 96, 2), O.max),
                     lambda: tt(A(m, 112, 120), A(m, 96, 112, 2), A(m, 97, 112, 2), O.max),
                     lambda: tt(ki, A(m, 112, 120), A("sm", 32 + 8 * h, 40 + 8 * h), O.max),
                     lambda: ts(A(dI, 8, 16), ki, 6, O.arith_shift_right, 63, O.bitwise_and),
                     lambda: ts(A(dI, 16, 24), ki, 63, O.bitwise_and),
-                    lambda: ts(A(dI, 0, 8), ki, 12, O.arith_shift_right, 15, O.bitwise_and),
-                    to_r]
+                    row_digit, to_r]
 
         def lines(h):
             lw = A("LWu", 8 * h, 8 * h + 8)
 
+            def same():
+                tt(H("eqe", h), H("SC5", h), RL[h], O.is_equal)
+                mm(CN[h], A("blk8", 0, 128), H("eqe", h), True, False)
+
+            def to_w():
+                ts(lw, A("SC5", 128 * h + 15, 128 * h + 128, 16), float(NONE1), O.min, -1.0, O.add)
+                act(H("Agl", h), IND(A("at", 0, 3200), lw), F.Copy)
+
             def draw():
-                tt(H("tt", h), IND(A("at", 0, 3200), lw), H("NVr", h), O.min)
+                tt(H("tt", h), H("Agl", h), H("b3", h), O.min)
                 act(H("t16", h), H("tt", h), F.Identity, bias=1.0 - 4096.0, scale=16384.0)
+
+            def payees():
+                if st > 0:
+                    cp(H("payf", h), IND(A("pt", 0, 3200), lw))
+                else:
+                    cp(H("payg", h), IND(A("pq", 0, 3200), lw))
+                    mm(H("b4", h, 128), A("row0", 0, 128), H("payg", h), True, True)
+                    act(H("payf", h), H("b4", h, 128), F.Copy)
+
+            def pay_r():
+                act(H("cm", h), H("payf", h), F.Identity, bias=-511.5 / 1024, scale=1.0 / 1024)
+                act(H("M1", h), H("cm", h), F.Identity, bias=MAGIC)
+                act(H("r8", h), H("M1", h), F.Identity, bias=-MAGIC - 8.0)
+
+            def one_hot():
+                ts(H("OH", h), CN[h], 8.0, O.min, PM, O.is_equal)
+                mm(OFF[h], A("woff", 0, 128), H("OH", h), True, False)
+
+            def product():
+                tt(H("prod", h), H("b3", h, 256), H("OH", h), O.mult)
+                mm(OFF[h], A("blk1", 0, 128), H("prod", h), False, True)
             return [lambda: tt(H("M5", h), RL[h], H("maskS", h), O.mult),
                     lambda: cp(H("Lu", h), RL[h]),
                     lambda: scan(H("SC5", h), H("rst", h), H("M5", h)),
-                    lambda: tt(H("eqe", h), H("SC5", h), RL[h], O.is_equal),
-                    lambda: ts(lw, A("SC5", 128 * h + 15, 128 * h + 128, 16), float(NONE1), O.min, -1.0, O.add),
-                    draw,
-                    lambda: cp(H("payf", h), IND(A("pt", 0, 3200), lw)),
-                    lambda: ts(H("r8", h), H("payf", h), 1.0 / 1024, O.mult, -511.5 / 1024 - 8.0, O.add)]
+                    same, to_w, draw, payees, pay_r,
+                    lambda: mm(CN[h], A("idB", 0, 128), H("r8", h), False, True),
+                    one_hot,
+                    lambda: scan(H("b3", h, 256), H("ones", h), H("OH", h), 0.0 if h == 0 else A("b3", 383, 384)),
+                    product]
+
+        def pairs5(h):
+            for a in range(7 if h == 0 else 15):
+                lo, c = max(128 * h, 16 * (a + 1)), 16 * a + 15
+                e = A("eqx", 256 * a + lo, 256 * a + 128 * h + 128)
+                ts(e, A("Lu", lo, 128 * h + 128), A("SC5", c, c + 1), O.is_equal)
+                mm(A(CN[h][1], lo - 128 * h, 128), A("blk8", 0, 128), e, False, False)
 
         def ge1(i):
             tt(A("ge1", i, D0, 16), A("Ag", i, D0, 16), A("b3", 128, XL), O.is_ge)
-            mm(A("b1", i, 128, 16), A("ge1", i, 2048, 16), A("bs64", 0, 8), False, i == 15)
-        best0, best1, lines0, lines1 = best(0), best(1), lines(0), lines(1)
-        weave([lambda i=i: ge1(i) for i in range(16)], best0[:6], 12)
-        weave(best1, best0[6:], 0)
-        for f in lines0[:6 if st == 0 else 8] + lines1[:5]:
+            mm(KI(1, i), A("ge1", i, 2048, 16), A("bs64", 0, 8), False, i >= 14)
+            if i == 15:
+                act(A("so1", 0, 64), KB[1][1], F.Copy)
+        best0, lines0, lines1 = best(0), lines(0), lines(1)
+        no_key = lambda: tt(A("sm", 32, 48), A("sm", 160, 176), A("sm", 176, 192), O.max)
+        weave([lambda i=i: ge1(i) for i in ODD], best0[:3] + [no_key] + best0[3:], 11)
+        for f in best(1):
             f()
-        pairs("SC5", 0, "Lu")
-        CN = (A("b6", 0, 128), A("b7", 0, 128))
-        mm(CN[0], A("blk8", 0, 128), H("eqe", 0), True, False)
-        mm(CN[1], A("blk8", 0, 128), H("eqe", 1), True, False)
-        for a in range(15):
-            if a < 7:
-                mm(A("b6", 16 * (a + 1), 128), A("blk8", 0, 128), A("eqx", 256 * a + 16 * (a + 1), 256 * a + 128), False, a == 6)
-            lo = max(128, 16 * (a + 1))
-            mm(A("b7", lo - 128, 128), A("blk8", 0, 128), A("eqx", 256 * a + lo, 256 * a + 256), False, a == 14)
-        if st == 0:
-            fill(A("pt", 3199, 3200), 8192)
-            lines0[6]()
-            lines0[7]()
-        for f in lines1[5:]:
-            f()
-        cum = lambda h: H("b3", h, 256)
-        OFF = (A("b5", 256, 384), A("b1", 256, 384))
+        act(A("b3", 0, 256), A("V2", 0, 256), F.Relu, scale=-1.0)
+        if not last:
+            fill(A("pq" if st == 0 else "pt", 3199, 3200), 8192)
+        calls = {"P0": lambda: pairs5(0), "P1": lambda: pairs5(1)}
+        for k in range(12):
+            calls["a%x" % k], calls["b%x" % k] = lines0[k], lines1[k]
+        for k in ORDER0 if st == 0 else ORDER:
+            calls[k]()
         for h in range(2):
-            tt(H("zz", h), CN[h], H("r8", h), O.add)
-        for h in range(2):
-            ts(H("OH", h), H("zz", h), 8.0, O.min, PM, O.is_equal)
-            mm(OFF[h], A("woff", 0, 128), H("OH", h), True, False)
-        scan(cum(0), H("ones", 0), H("OH", 0))
-        tt(H("prod", 0), cum(0), H("OH", 0), O.mult)
-        scan(cum(1), H("ones", 1), H("OH", 1), A("b3", 383, 384))
-        mm(OFF[0], A("blk1", 0, 128), H("prod", 0), False, True)
-        tt(H("prod", 1), cum(1), H("OH", 1), O.mult)
-        mm(OFF[1], A("blk1", 0, 128), H("prod", 1), False, True)
-        for h in range(2):
-            act(H("b3", h, 256), CN[h], F.Relu, bias=9.0, scale=-1.0)
+            act(H("sgn", h), CN[h], F.Sign, bias=7.5, scale=-1.0)
+            act(H("b3", h, 256), H("sgn", h), F.Relu)
         tm = A("b3", 0, 256)
         tt(H("M6", 0), OFF[0], H("maskS", 0), O.mult)
         tt(H("M6", 1), OFF[1], H("maskS", 1), O.mult)
@@ -434,14 +473,14 @@ def rank_program(g, core, T, topo):
         cp(A("OWu", 0, 16), o6)
         tt(IND(A(win, 0, WIN), A("OWu", 0, 16)), A("t16", 0, 256), A("payf", 0, 256), O.add)
         sync_for(P, "g", [(win, 0, WIN, 1)], [])
-        calls = plan(topo, T.cores, me)
-        for c in calls:
+        sends = plan(topo, T.cores, me)
+        for c in sends:
             g.remote_dma_fused([RemoteDMATransfer(
                 dst_ids=[DstId(rid=topo.addr(T.cores[r], core)[0], pnc=topo.addr(T.cores[r], core)[1])],
                 dma_engine_mask=sum(1 << e for e in engines), remote_sem=T.sem["arr%d" % st],
                 src=T[win][:, 256 * r + 1:256 * r + 33], dst=T[land][:, 32 * me:32 * me + 32])
                 for r, engines in c], local_sem=T.sem["loc"])
-        out_n = sum(len(e) for c in calls for r, e in c)
+        out_n = sum(len(e) for c in sends for r, e in c)
         arrive = sum(len(e) for q in range(8) if q != me for c in plan(topo, T.cores, q) for r, e in c if r == me)
         for q in range(8):
             if q != me:
@@ -455,9 +494,8 @@ def rank_program(g, core, T, topo):
             tt(A("OHu", 0, 256), A("b6", 256, 512), A("UI", 0, 256), O.is_equal)
         cp(A("boU", 0, 16), A("sm", 80, 96))
         if not last:
-            act(A("Agl", 0, 256), IND(A("at", 0, 3200), A("LWu", 0, 16)), F.Copy)
             for h in range(2):
-                act(H("b7", h, 128), CN[h], F.Relu, bias=N9, scale=NNEG)
+                act(H("b7", h, 128), H("sgn", h), F.Relu, scale=NONEC)
             ts(A("sm", 96, 112), o6, 2048.5, O.is_gt)
             ts(A("sm", 112, 128), l5, float(NONE1), O.min, -1.0, O.add)
         cp(IND(A("vt", 0, 1296), A("boU", 0, 16)), A("Vn", 0, 256))
@@ -489,7 +527,7 @@ def rank_program(g, core, T, topo):
     y.dma_start(T.yw[:], T.ywS[0:128:16, 0:256]).then_inc(T.sem["dyw"], 16)
     for sem in ("sv", "ss", "sp", "sg"):
         g.wait_ge(T.sem[sem], P["cnt"][sem])
-    for sem in ("dwk", "dvp", "dqu", "dam", "dyv", "dyw", "dyc"):
+    for sem in ("dwk", "dvp", "dqu", "dam", "dpq", "dyv", "dyw", "dyc"):
         g.wait_ge(T.sem[sem], 16)
     g.wait_ge(T.sem["dpay"], 256)
     g.wait_ge(T.sem["loc"], 3 * out_n)

from concourse.bass import DstId, RemoteDMATransfer
from concourse.mybir import AluOpType as O, ActivationFunctionType as F

WIN = 2312
SCRATCH = {}
for _n in "wkb ci xi".split():
    SCRATCH[_n] = ("sbuf", [128, 256], "int32")
for _n in "wkf xz UI M1 M5 M6 SC5 SC6 t16 payf payg OHu UIn ywS cm land0 land1 land2".split():
    SCRATCH[_n] = ("sbuf", [128, 256], "float32")
for _n in "maskS rst ones V1 V2 NVr eqd eqe tt r8 sgn OH prod Vn An Agl cB".split():
    SCRATCH[_n] = ("sbuf", [128, 256], "bfloat16")
for _n in "blk1 blkT blk8 woff idB selb selL selC TTs0 TTs1".split():
    SCRATCH[_n] = ("sbuf", [128, 128], "bfloat16")
for _n in "BWu LWu OWu boU aoU".split():
    SCRATCH[_n] = ("sbuf", [128, 16], "uint16")
for _n in "xu Lu Uo".split():
    SCRATCH[_n] = ("sbuf", [128, 256], "uint16")
for _n in "NVx ge0 Ag ge1".split():
    SCRATCH[_n] = ("sbuf", [128, 2048], "bfloat16")
for _n in "onesF idF sel8 selT row0".split():
    SCRATCH[_n] = ("sbuf", [128, 128], "float32")
for _n in range(3):
    SCRATCH["win%d" % _n] = ("sbuf", [128, WIN], "float32")
for _n in range(8):
    SCRATCH["b%d" % _n] = ("psum", [128, 512], "float32")
for _n in range(2):
    SCRATCH["so%d" % _n] = ("sbuf", [128, 64], "float32")
    SCRATCH["mx%d" % _n] = ("sbuf", [128, 128], "float32")
    SCRATCH["ki%d" % _n] = ("sbuf", [128, 8], "int32")
    SCRATCH["digI%d" % _n] = ("sbuf", [128, 24], "int32")
    SCRATCH["digB%d" % _n] = ("sbuf", [128, 32], "bfloat16")
SCRATCH["quS"] = ("sbuf", [128, 1032], "int32")
SCRATCH["ut"] = ("sbuf", [128, 1296], "float32")
SCRATCH["vt"] = ("sbuf", [128, 1296], "bfloat16")
SCRATCH["at"] = ("sbuf", [128, 3456], "bfloat16")
SCRATCH["pt"] = ("sbuf", [128, 3200], "int32")
SCRATCH["pq"] = ("sbuf", [128, 3200], "int32")
SCRATCH["eqx"] = ("sbuf", [128, 3840], "bfloat16")
SCRATCH["l15"] = ("sbuf", [128, 256], "int32")
SCRATCH["l4"] = ("sbuf", [128, 128], "int32")
SCRATCH["l16"] = ("sbuf", [128, 16], "int32")
SCRATCH["pci"] = ("sbuf", [128, 8], "int32")
SCRATCH["col"] = ("sbuf", [128, 32], "float32")
SCRATCH["bs64"] = ("sbuf", [128, 8], "bfloat16")
SCRATCH["dumpA"] = ("sbuf", [128, 16], "float32")
SCRATCH["dumpB"] = ("sbuf", [128, 16], "float32")
SCRATCH["sm"] = ("sbuf", [128, 192], "float32")
SEMAPHORES = ["sv", "ss", "sp", "sg", "dwk", "dvp", "dqu", "dam", "dpq", "dpay", "dyv", "dyw", "dyc", "loc", "arr0", "arr1", "arr2"]
NONE1 = 3200
XKEY = 272 * 4096 + NONE1
LOW = 2097152
HALF = (XKEY + LOW) / 2.0
MAGIC = 12582912.0
XL = 224
NV = 5
ODD = list(range(1, 16, 2)) + list(range(0, 16, 2))
ORDER0 = "a0 a1 a2 a4 a6 a7 a3 P0 a8 b0 b1 b2 b4 b6 b7 b3 P1 b8 a9 aa a5 ab b5 b9 ba bb".split()
ORDER = "a0 a1 a2 a3 a4 P0 a6 a7 a8 b0 b1 b2 b3 b4 P1 b6 b7 b8 a9 aa a5 ab b5 b9 ba bb".split()


def A(name, c0, c1, step=1, p0=0, p1=128):
    return ("A", name, c0, c1, step, p0, p1)


def IND(win, off):
    return ("I", win, off)


KB = ((A("b0", 0, 64), A("b5", 384, 448)), (A("b1", 0, 64), A("b6", 128, 192)))


def KI(h, i):
    k = KB[h][i % 2]
    return A(k[1], k[2] + i // 2, k[3], 8)


def is_view(x):
    return isinstance(x, tuple) and len(x) > 0 and (x[0] == "A" or x[0] == "I")


def hits(a, b):
    if a[2] <= b[1] or b[2] <= a[1]:
        return False
    return not (a[3] > 1 and a[3] == b[3] and (a[1] - b[1]) % a[3] != 0)


def is_psum(name):
    return len(name) == 2 and name[0] == "b"


def resolve(P, x):
    if x[0] == "I":
        return resolve(P, x[1]).indirect(resolve(P, x[2]))
    t = P["T"][x[1]]
    if x[4] == 1:
        return t[x[5]:x[6], x[2]:x[3]]
    return t[x[5]:x[6], x[2]:x[3]:x[4]]


def regions(views):
    out = []
    for v in views:
        if v[0] == "I":
            out += regions([v[1], v[2]])
        else:
            out.append((v[1], v[2], v[3], v[4]))
    return out


def sync_for(P, q, reads, writes):
    need = []
    for kind, regs in (("r", reads), ("w", writes)):
        for r in regs:
            ps = is_psum(r[0])
            for hk, hr, hq, sem, val, clock in P["hist"].get(r[0], []):
                same = hq == q
                if same or not ps:
                    if (hk == "r" and (kind == "r" or same)) or (same and kind == "w" and q == "p") or not hits(r, hr):
                        continue
                need.append((sem, val, clock))
    best = {}
    for sem, val, clock in need:
        if P["known"][q].get(sem, 0) < val and (sem not in best or best[sem][0] < val):
            best[sem] = (val, clock)
    for sem in list(best):
        if any(s2 != sem and best[s2][1].get(sem, 0) >= best[sem][0] for s2 in best):
            del best[sem]
    for sem in best:
        val, clock = best[sem]
        P["eng"][q].wait_ge(P["T"].sem[sem], val)
        k = P["known"][q]
        for s2, v2 in clock.items():
            if k.get(s2, 0) < v2:
                k[s2] = v2


def note(P, q, reads, writes, sem, val):
    clock = dict(P["known"].get(q, {}))
    clock[sem] = max(val, clock.get(sem, 0))
    for kind, regs in (("r", reads), ("w", writes)):
        for r in regs:
            lst = P["hist"].setdefault(r[0], [])
            if kind == "w" and r[3] == 1:
                lst[:] = [h for h in lst if not (h[2] == q and r[1] <= h[1][1] and h[1][2] <= r[2])]
            lst.append((kind, r, q, sem, val, clock))


SEM_OF = {"v": "sv", "s": "ss", "p": "sp", "g": "sg"}


def op(P, q, fn, out, *args, **kw):
    reads = regions([a for a in args if is_view(a)] + [a for a in kw.values() if is_view(a)])
    if out[0] == "I":
        writes = regions([out[1]])
        reads += regions([out[2]])
    else:
        writes = regions([out])
    sync_for(P, q, reads, writes)
    sem = SEM_OF[q]
    P["cnt"][sem] += 1
    fn(resolve(P, out), *[resolve(P, a) if is_view(a) else a for a in args],
       **{k: (resolve(P, a) if is_view(a) else a) for k, a in kw.items()}).then_inc(P["T"].sem[sem], 1)
    note(P, q, reads, writes, sem, P["cnt"][sem])


def weave(first, second, start):
    second = list(second)
    for n, f in enumerate(first):
        f()
        if n >= start and second:
            second.pop(0)()
    for f in second:
        f()


def rank_program(g, core, T, topo):
    me = T.rank_of(core)
    if me is None:
        return
    v, s, pe, y = g.vector, g.scalar, g.tensor, g.sync
    P = {"T": T, "hist": {}, "known": {q: {} for q in "vspyg"}, "cnt": {"sv": 0, "ss": 0, "sp": 0, "sg": 0},
         "eng": {"v": v, "s": s, "p": pe, "y": y, "g": g}}

    def cp(out, in_): op(P, "v", v.tensor_copy, out, in_)
    def tt(out, a, b, o): op(P, "v", v.tensor_tensor, out, a, b, o)
    def ts(out, a, s1, o1, s2=None, o2=None):
        if o2 is None:
            op(P, "v", v.tensor_scalar, out, a, s1, None, o1)
        else:
            op(P, "v", v.tensor_scalar, out, a, s1, s2, o1, o2)
    def scan(out, d0, d1, ini=0.0): op(P, "v", v.tensor_tensor_scan, out, d0, d1, ini, O.mult, O.add)
    def fill(out, c): op(P, "v", v.memset, out, c)
    def act(out, in_, f, **kw): op(P, "s", s.activation, out, in_, f, **kw)
    def mm(out, l, r, st, sp): op(P, "p", pe.matmul, out, l, r, st, sp)
    def iota(out, pat, base, cm, **kw): op(P, "g", g.iota, out, pat, base, cm, **kw)
    def pick(out, in_, pat, cmp, base, cm): op(P, "g", g.affine_select, out, in_, pat, cmp, 0.0, base, cm)
    def H(name, h, c0=0): return A(name, c0 + 128 * h, c0 + 128 * h + 128)
    def C(k, n=128): return A("col", k, k + 1, 1, 0, n)

    def load(q, out, src, sem):
        P["eng"][q].dma_start(resolve(P, out), src).then_inc(T.sem[sem], 16)
        note(P, "d" + sem, [], regions([out]), sem, 16)
    load("y", A("wkb", 0, 256, 1, 0, 8), T.wk[:], "dwk")
    load("s", A("vt", 0, 1024), T.vp[:], "dvp")
    load("y", A("quS", 0, 1024), T.qu[:], "dqu")
    load("y", A("at", 0, 3200), T.am[:], "dam")

    imp = {"allow_small_or_imprecise_dtypes": True}
    iota(A("pci", 0, 1), [[1, 1]], 0, 1)
    iota(A("l15", 0, 256), [[0, 16], [1, 16]], 0, 0)
    iota(A("onesF", 0, 128), [[0, 128]], 1, 0, **imp)
    pick(A("selT", 0, 128, 1, 0, 8), A("onesF", 0, 128, 1, 0, 8), [[1, 128]], O.is_ge, 0, -16)
    pick(A("sel8", 0, 128, 1, 0, 8), A("selT", 0, 128, 1, 0, 8), [[-1, 128]], O.is_ge, 15, 16)
    iota(A("l4", 0, 128), [[1, 8], [0, 16]], 0, 0)
    iota(A("l16", 0, 16), [[16, 16]], 0, 0)
    iota(A("ones", 0, 256), [[0, 256]], 1, 0, **imp)
    pick(A("blkT", 0, 128), A("ones", 0, 128), [[-16, 8], [0, 16]], O.is_ge, 0, 1)
    pick(A("blk1", 0, 128), A("blkT", 0, 128), [[16, 8], [0, 16]], O.is_ge, 15, -1)
    pick(A("idF", 0, 128), A("onesF", 0, 128), [[-1, 128]], O.is_equal, 0, 1)
    pick(A("row0", 0, 128), A("onesF", 0, 128), [[-16, 8], [0, 16]], O.is_equal, 0, 1)
    pick(A("idB", 0, 128), A("ones", 0, 128), [[-1, 128]], O.is_equal, 0, 1)
    iota(A("pq", 0, 3200), [[0, 3200]], 0, 0)
    sync_for(P, "y", [], [("pq", 0, 3200, 1)])
    y.dma_start(T.pq[0:128:16, :], T.pay[:]).then_inc(T.sem["dpq"], 16)
    note(P, "dpq", [], [("pq", 0, 3200, 1)], "dpq", 16)
    for j in range(16):
        y.dma_start(T.pt[j:128:16, :], T.pay[:]).then_inc(T.sem["dpay"], 16)
    note(P, "dpay", [], [("pt", 0, 3200, 1)], "dpay", 256)
    for k in range(3):
        for r in range(8):
            iota(A("win%d" % k, 256 * r + 1, 256 * r + 33), [[0, 32]], 1024 * r + 1025 - 4096, 0, **imp)
    p0 = A("pci", 0, 1)
    ts(A("pci", 1, 2), p0, 15, O.bitwise_and)
    ts(A("pci", 2, 3), p0, 3, O.arith_shift_right)
    ts(A("pci", 3, 4), p0, 7, O.bitwise_and)
    cp(A("col", 0, 4), A("pci", 0, 4))
    PM, PD = C(1), C(2)
    ADD1, NONEC, J256, NEG = C(4), C(5), C(8), C(9)
    maskP = lambda h: H("b2", h)
    SC = lambda h: H("b2", h, 256)
    ts(A("b2", 0, 256), A("l15", 0, 256), PM, O.is_equal)
    ts(A("rst", 0, 256), A("l15", 0, 256), 0.0, O.not_equal)
    ts(NEG, PM, -4096.0, O.mult, -1.0, O.add)
    ts(ADD1, PM, 4096.0, O.mult, 1.0, O.add)
    ts(NONEC, PM, 4096.0, O.mult, float(NONE1), O.add)
    ts(A("ut", 1024, 1032), A("l15", 0, 8), 0.0, O.mult, NONEC, O.add)
    fill(A("quS", 1024, 1032), NONE1 - 1)
    fill(A("vt", 1024, 1040), 0.0)
    for a in list(range(7)) + list(range(8, 15)):
        fill(A("eqx", 256 * a + (0 if a < 7 else 128), 256 * a + 16 * (a + 1)), 0.0)
    blksel = A("blk1", 0, 128, 16)

    def late_constants():
        ts(A("maskS", 0, 256), A("l15", 0, 256), PM, O.is_equal)
        ts(J256, PM, 256.0, O.mult)
        ts(C(10), PD, 0.0, O.is_equal, 4096.0, O.mult)
        ts(C(11), PD, 1.0, O.is_equal, 64.0, O.mult)
        ts(C(12), PD, 2.0, O.is_equal)
        ts(C(13), PD, 3.0, O.is_equal, 8192.0, O.mult)
        ts(A("selb", 0, 128, 1, 0, 32), A("l4", 0, 128, 1, 0, 32), C(3, 32), O.is_equal)
        tt(C(14), C(11), C(12), O.add)
        ts(A("dumpB", 0, 16), A("l16", 0, 16), PM, O.add, 1025.0, O.add)
        ts(A("dumpA", 0, 16), A("l16", 0, 16), PM, O.add, 3200.0, O.add)
        tt(C(15), C(14), C(13), O.add)
        tt(C(16), C(14), C(10), O.add)

    def late_scalar():
        act(A("bs64", 0, 8), blksel, F.Copy, scale=65536.0)
        act(A("blk8", 0, 128), A("blk1", 0, 128), F.Copy, scale=8.0)
        act(A("woff", 0, 128), A("blk1", 0, 128), F.Copy, scale=J256)
        act(A("selL", 0, 128, 1, 0, 32), A("selb", 0, 128, 1, 0, 32), F.Copy, scale=C(15, 32))
        act(A("selC", 0, 128, 1, 0, 32), A("selb", 0, 128, 1, 0, 32), F.Copy, scale=C(16, 32))

    def pairs1():
        for a in range(15):
            c = 256 + 16 * a + 15
            ts(A("eqx", 256 * a + 16 * (a + 1), 256 * a + 256), A("xu", 16 * (a + 1), 256), A("b2", c, c + 1), O.is_equal)

    for st in range(3):
        last = st == 2
        win, land = "win%d" % st, "land%d" % st
        base = 1 if st == 0 else 1 + 1024 * me
        x = "xz" if st == 0 else "xi"
        if st == 0:
            ts(A("wkf", 0, 256, 1, 0, 8), A("wkb", 0, 256, 1, 0, 8), 1.0, O.add)
            mm(A("b4", 256, 512), A("sel8", 0, 128, 1, 0, 8), A("wkf", 0, 256, 1, 0, 8), True, True)
            late_constants()
            for h in range(2):
                cp(H("xz", h), H("b4", h, 256))
        else:
            old = "land%d" % (st - 1)
            act(A("cm", 0, 256), A(old, 0, 256), F.Identity, bias=MAGIC, scale=1.0 / 16384)
            act(A("cB", 0, 256), A("cm", 0, 256), F.Identity, bias=-MAGIC)
            for h in range(2):
                ts(H("ci", h), H(old, h), 4096.0, O.add)
            for h in range(2):
                ts(H("xi", h), H("ci", h), 16383, O.bitwise_and)
        for h in range(2):
            tt(H("M1", h), H(x, h), maskP(h), O.mult)
        for h in range(2):
            scan(SC(h), H("rst", h), H("M1", h))
        scW = A("b2", 256 + 15, 512, 16)
        ts(A("BWu", 0, 16), scW, float(-base), O.add)
        BW = A("BWu", 0, 16)

        def eqd1(h):
            tt(H("eqd", h), SC(h), H(x, h), O.is_equal)
        if st == 0:
            cp(A("V2", 0, 256), IND(A("vt", 0, 1040), BW))
            for h in range(2):
                cp(H("xu", h), H(x, h))
            for h in range(2):
                eqd1(h)
            pairs1()
            cp(A("Uo", 0, 256), IND(A("quS", 0, 1032), BW))
            ts(A("ut", 0, 1024), A("quS", 0, 1024), ADD1, O.add)
            late_scalar()
        else:
            act(A("UI", 0, 256), IND(A("ut", 0, 1032), BW), F.Copy)
            tt(A("V1", 0, 256), IND(A("vt", 0, 1040), BW), A("cB", 0, 256), O.subtract)
            cp(H("xu", 0), H(x, 0))
            ts(A("V2", 0, 256), A("V1", 0, 256), -255.0, O.max)
            ts(A("Uo", 0, 256), A("UI", 0, 256), NEG, O.add)
            cp(H("xu", 1), H(x, 1))
            for h in range(2):
                eqd1(h)
            pairs1()
        for i in range(16 - NV):
            act(A("NVx", i, 2048, 16), A("V2", 0, 128), F.Copy, scale=-1.0)
        for i in range(16 - NV, 16):
            ts(A("NVx", i, 2048, 16), A("V2", 0, 128), -1.0, O.mult)
        act(A("NVr", 0, 256), A("V2", 0, 256), F.Relu, scale=-1.0)
        if st == 0:
            act(A("UI", 0, 256), IND(A("ut", 0, 1032), BW), F.Copy)
        act(A("b3", 128, XL), A("V2", 128, XL), F.Copy, scale=-1.0)
        for c0, c1 in ((XL, 256), (128, 176), (176, XL)):
            act(A("Ag", 16 * (c0 - 128), 16 * (c1 - 128)), IND(A("at", 0, 3200), A("Uo", c0, c1)), F.Copy)
        for h in range(2):
            for e in range(2):
                mm(KB[h][e], H("UI", h), A("idF", e, 128, 2), True, False)
        for h in range(2):
            mm(A("b4", 8 * h, 8 * h + 8), H("NVr", h), blksel, True, True)
        for h in range(2):
            out = A("b4", 16 + 8 * h, 24 + 8 * h)
            mm(out, H("eqd", h), blksel, True, False)
            n = 7 if h == 0 else 15
            for a in range(n):
                mm(out, H("eqx", h, 256 * a), blksel, False, a == n - 1)
        D0 = 16 * (XL - 128)
        mm(A("b7", 0, 512), A("idB", 0, 128), A("Ag", D0, 2048), True, False)
        for i in range(16):
            mm(A("b7", i, 512, 16), A("idB", 0, 128), A("V2", XL, 256), False, i == 15)
        act(A("ge1", D0, 2048), A("b7", 0, 512), F.Sign, bias=0.5)
        tt(A("ge0", 0, 2048), IND(A("at", 0, 3200), A("Uo", 0, 128)), A("NVx", 0, 2048), O.is_ge)
        for i in ODD:
            mm(KI(0, i), A("ge0", i, 2048, 16), A("bs64", 0, 8), False, i >= 14)
        act(A("so0", 0, 64), KB[0][1], F.Copy)
        act(A("sm", 0, 16), A("b4", 0, 16), F.Sign, bias=-0.5)
        act(A("sm", 16, 32), A("b4", 16, 32), F.Sign, bias=-1.5)
        for h in range(2):
            act(A("digB%d" % h, 24, 32), A("sm", 16 + 8 * h, 24 + 8 * h), F.Relu)
        act(A("sm", 160, 176), A("sm", 0, 16), F.Identity, bias=HALF - LOW, scale=-HALF)
        act(A("sm", 176, 192), A("sm", 16, 32), F.Identity, bias=HALF - LOW, scale=HALF)
        RL = (H("b5", 0), A("b0", 128, 256))
        CN = (A("b6", 0, 128), A("b7", 0, 128))
        OFF = (A("b5", 256, 384), A("b1", 256, 384))

        def best(h):
            m = "mx%d" % h
            ki, dI, dB, tp = A("ki%d" % h, 0, 8), "digI%d" % h, "digB%d" % h, A("b4", 128 + 128 * h, 256 + 128 * h, 1, 0, 32)
            tr = A("TTs%d" % h, 0, 128, 1, 0, 32)

            def row_digit():
                if not last:
                    ts(A(dI, 0, 8), ki, 12, O.arith_shift_right, 15, O.bitwise_and)

            def to_r():
                cp(A(dB, 0, 24), A(dI, 0, 24))
                mm(tp, A(dB, 0, 32), A("idB", 0, 128), True, True)
                act(tr, tp, F.Copy)
                mm(RL[h], A("selL", 0, 128, 1, 0, 32), tr, True, True)
                if not last:
                    mm(H("b6", h, 256), A("selC", 0, 128, 1, 0, 32), tr, True, True)
            return [lambda: tt(A(m, 0, 64), KB[h][0], A("so%d" % h, 0, 64), O.max),
                    lambda: tt(A(m, 64, 96), A(m, 0, 64, 2), A(m, 1, 64, 2), O.max),
                    lambda: tt(A(m, 96, 112), A(m, 64, 96, 2), A(m, 65, 96, 2), O.max),
                    lambda: tt(A(m, 112, 120), A(m, 96, 112, 2), A(m, 97, 112, 2), O.max),
                    lambda: tt(ki, A(m, 112, 120), A("sm", 32 + 8 * h, 40 + 8 * h), O.max),
                    lambda: ts(A(dI, 8, 16), ki, 6, O.arith_shift_right, 63, O.bitwise_and),
                    lambda: ts(A(dI, 16, 24), ki, 63, O.bitwise_and),
                    row_digit, to_r]

        def lines(h):
            lw = A("LWu", 8 * h, 8 * h + 8)

            def same():
                tt(H("eqe", h), H("SC5", h), RL[h], O.is_equal)
                mm(CN[h], A("blk8", 0, 128), H("eqe", h), True, False)

            def to_w():
                ts(lw, A("SC5", 128 * h + 15, 128 * h + 128, 16), float(NONE1), O.min, -1.0, O.add)
                act(H("Agl", h), IND(A("at", 0, 3200), lw), F.Copy)

            def draw():
                tt(H("tt", h), H("Agl", h), H("b3", h), O.min)
                act(H("t16", h), H("tt", h), F.Identity, bias=1.0 - 4096.0, scale=16384.0)

            def payees():
                if st > 0:
                    cp(H("payf", h), IND(A("pt", 0, 3200), lw))
                else:
                    cp(H("payg", h), IND(A("pq", 0, 3200), lw))
                    mm(H("b4", h, 128), A("row0", 0, 128), H("payg", h), True, True)
                    act(H("payf", h), H("b4", h, 128), F.Copy)

            def pay_r():
                act(H("cm", h), H("payf", h), F.Identity, bias=-511.5 / 1024, scale=1.0 / 1024)
                act(H("M1", h), H("cm", h), F.Identity, bias=MAGIC)
                act(H("r8", h), H("M1", h), F.Identity, bias=-MAGIC - 8.0)

            def one_hot():
                ts(H("OH", h), CN[h], 8.0, O.min, PM, O.is_equal)
                mm(OFF[h], A("woff", 0, 128), H("OH", h), True, False)

            def product():
                tt(H("prod", h), H("b3", h, 256), H("OH", h), O.mult)
                mm(OFF[h], A("blk1", 0, 128), H("prod", h), False, True)
            return [lambda: tt(H("M5", h), RL[h], H("maskS", h), O.mult),
                    lambda: cp(H("Lu", h), RL[h]),
                    lambda: scan(H("SC5", h), H("rst", h), H("M5", h)),
                    same, to_w, draw, payees, pay_r,
                    lambda: mm(CN[h], A("idB", 0, 128), H("r8", h), False, True),
                    one_hot,
                    lambda: scan(H("b3", h, 256), H("ones", h), H("OH", h), 0.0 if h == 0 else A("b3", 383, 384)),
                    product]

        def pairs5(h):
            for a in range(7 if h == 0 else 15):
                lo, c = max(128 * h, 16 * (a + 1)), 16 * a + 15
                e = A("eqx", 256 * a + lo, 256 * a + 128 * h + 128)
                ts(e, A("Lu", lo, 128 * h + 128), A("SC5", c, c + 1), O.is_equal)
                mm(A(CN[h][1], lo - 128 * h, 128), A("blk8", 0, 128), e, False, False)

        def ge1(i):
            tt(A("ge1", i, D0, 16), A("Ag", i, D0, 16), A("b3", 128, XL), O.is_ge)
            mm(KI(1, i), A("ge1", i, 2048, 16), A("bs64", 0, 8), False, i >= 14)
            if i == 15:
                act(A("so1", 0, 64), KB[1][1], F.Copy)
        best0, lines0, lines1 = best(0), lines(0), lines(1)
        no_key = lambda: tt(A("sm", 32, 48), A("sm", 160, 176), A("sm", 176, 192), O.max)
        weave([lambda i=i: ge1(i) for i in ODD], best0[:3] + [no_key] + best0[3:], 11)
        for f in best(1):
            f()
        act(A("b3", 0, 256), A("V2", 0, 256), F.Relu, scale=-1.0)
        if not last:
            fill(A("pq" if st == 0 else "pt", 3199, 3200), 8192)
        calls = {"P0": lambda: pairs5(0), "P1": lambda: pairs5(1)}
        for k in range(12):
            calls["a%x" % k], calls["b%x" % k] = lines0[k], lines1[k]
        for k in ORDER0 if st == 0 else ORDER:
            calls[k]()
        for h in range(2):
            act(H("sgn", h), CN[h], F.Sign, bias=7.5, scale=-1.0)
            act(H("b3", h, 256), H("sgn", h), F.Relu)
        tm = A("b3", 0, 256)
        tt(H("M6", 0), OFF[0], H("maskS", 0), O.mult)
        tt(H("M6", 1), OFF[1], H("maskS", 1), O.mult)
        for h in range(2):
            scan(H("SC6", h), H("rst", h), H("M6", h))
        o6, l5 = A("SC6", 15, 256, 16), A("SC5", 15, 256, 16)
        ts(A("sm", 64, 80), scW, float(-base), O.add)
        ts(A("sm", 48, 64), l5, 4096.0, O.is_gt)
        cp(A("OWu", 0, 16), o6)
        tt(IND(A(win, 0, WIN), A("OWu", 0, 16)), A("t16", 0, 256), A("payf", 0, 256), O.add)
        sync_for(P, "g", [(win, 0, WIN, 1)], [])
        sends = plan(topo, T.cores, me)
        for c in sends:
            g.remote_dma_fused([RemoteDMATransfer(
                dst_ids=[DstId(rid=topo.addr(T.cores[r], core)[0], pnc=topo.addr(T.cores[r], core)[1])],
                dma_engine_mask=sum(1 << e for e in engines), remote_sem=T.sem["arr%d" % st],
                src=T[win][:, 256 * r + 1:256 * r + 33], dst=T[land][:, 32 * me:32 * me + 32])
                for r, engines in c], local_sem=T.sem["loc"])
        out_n = sum(len(e) for c in sends for r, e in c)
        arrive = sum(len(e) for q in range(8) if q != me for c in plan(topo, T.cores, q) for r, e in c if r == me)
        for q in range(8):
            if q != me:
                note(P, "remote", [], [(land, 32 * q, 32 * q + 32, 1)], "arr%d" % st, arrive)
        cp(A(land, 32 * me, 32 * me + 32), A(win, 256 * me + 1, 256 * me + 33))
        tt(tm, A("b3", 256, 512), A("tt", 0, 256), O.mult)
        tt(A("sm", 48, 64), A("sm", 48, 64), A("dumpB", 0, 16), O.mult)
        tt(A("Vn", 0, 256), tm, A("V2", 0, 256), O.add)
        tt(A("sm", 80, 96), A("sm", 48, 64), A("sm", 64, 80), O.max)
        if not last:
            tt(A("OHu", 0, 256), A("b6", 256, 512), A("UI", 0, 256), O.is_equal)
        cp(A("boU", 0, 16), A("sm", 80, 96))
        if not last:
            for h in range(2):
                act(H("b7", h, 128), H("sgn", h), F.Relu, scale=NONEC)
            ts(A("sm", 96, 112), o6, 2048.5, O.is_gt)
            ts(A("sm", 112, 128), l5, float(NONE1), O.min, -1.0, O.add)
        cp(IND(A("vt", 0, 1296), A("boU", 0, 16)), A("Vn", 0, 256))
        if last:
            break
        okX = A("b7", 128, 384)
        tt(okX, okX, A("OHu", 0, 256), O.mult)
        tt(A("sm", 128, 144), A("sm", 96, 112), A("dumpA", 0, 16), O.mult)
        tt(A("UIn", 0, 256), A("UI", 0, 256), okX, O.max)
        tt(A("sm", 144, 160), A("sm", 128, 144), A("sm", 112, 128), O.max)
        tt(A("An", 0, 256), A("Agl", 0, 256), tm, O.subtract)
        cp(A("aoU", 0, 16), A("sm", 144, 160))
        cp(IND(A("ut", 0, 1296), A("boU", 0, 16)), A("UIn", 0, 256))
        cp(IND(A("at", 0, 3456), A("aoU", 0, 16)), A("An", 0, 256))

    sync_for(P, "y", [("vt", 0, 1024, 1)], [])
    y.dma_start(T.yv[:], T.vt[:, 0:1024]).then_inc(T.sem["dyv"], 16)
    act(A("cm", 0, 256), A("land2", 0, 256), F.Identity, bias=MAGIC, scale=1.0 / 16384)
    act(A("cB", 0, 256), A("cm", 0, 256), F.Identity, bias=-MAGIC)
    for h in range(2):
        ts(H("ci", h), H("land2", h), 4096.0, O.add)
    for h in range(2):
        ts(H("xi", h), H("ci", h), 16383, O.bitwise_and)
    for h in range(2):
        ts(H("ywS", h), H("xi", h), float(-(1 + 1024 * me)), O.add)
    sync_for(P, "s", regions([A("cB", 0, 256)]), [])
    s.dma_start(T.yc[:], T.cB[:, 0:256]).then_inc(T.sem["dyc"], 16)
    sync_for(P, "y", regions([A("ywS", 0, 256)]), [])
    y.dma_start(T.yw[:], T.ywS[0:128:16, 0:256]).then_inc(T.sem["dyw"], 16)
    for sem in ("sv", "ss", "sp", "sg"):
        g.wait_ge(T.sem[sem], P["cnt"][sem])
    for sem in ("dwk", "dvp", "dqu", "dam", "dpq", "dyv", "dyw", "dyc"):
        g.wait_ge(T.sem[sem], 16)
    g.wait_ge(T.sem["dpay"], 256)
    g.wait_ge(T.sem["loc"], 3 * out_n)
    for k in range(3):
        g.wait_ge(T.sem["arr%d" % k], arrive)


def plan(topo, cores, q):
    src = cores[q]
    others = [(q + k) % len(cores) for k in range(1, len(cores))]
    near = [r for r in others if cores[r] in topo.cores_of(src)]
    far = [r for r in others if r not in near]
    far.sort(key=lambda r: topo.same_plane(src, cores[r]) or topo.mates(src, cores[r]))
    out = [e for e in topo.engines(src, cores[far[0]])]
    inside = [e for e in topo.engines(src, cores[near[0]]) if e not in out]
    n = len(out) // 4
    first = [(r, out[n * k:n * k + n]) for k, r in enumerate(far[:4])]
    first += [(r, inside[n * k:n * k + n]) for k, r in enumerate(near)]
    m = len(out) // 2
    return [first, [(r, out[m * k:m * k + m]) for k, r in enumerate(far[4:])]]
